import numpy as np
import ml_dtypes


def mxq(x, axis, fmt="e4m3"):
    dtype, down = {"e4m3": (ml_dtypes.float8_e4m3fn, 7), "e5m2": (ml_dtypes.float8_e5m2, 14)}[fmt]
    v = np.moveaxis(np.asarray(x, np.float32).astype(ml_dtypes.bfloat16).astype(np.float64), axis, -1)
    blocks = v.reshape(v.shape[:-1] + (-1, 32))
    amax = np.abs(blocks).max(-1, keepdims=True)
    byte = np.maximum(np.where(amax > 0, np.frexp(amax)[1] - 1 + 127, 0) - down, 1)
    scale = np.exp2(byte - 127.0)
    codes = (blocks / scale).astype(np.float32).astype(dtype).astype(np.float64)
    return np.moveaxis((codes * scale).reshape(v.shape), -1, axis)


WIDE = False


def mx_kscale(k):
    if not WIDE:
        return np.ones(k)
    levels = np.array([10, -10, 5, -5, 0])
    if k % 512:
        return np.exp2(np.random.permutation(np.resize(levels, k // 32))).repeat(32)
    a = np.empty((k // 512, 16))
    for p in range(k // 512):
        a[p, :8] = np.random.permutation(np.resize(levels, 8))
        for g in range(8):
            far = levels[np.abs(levels - a[p, g]) >= 10]
            a[p, g + 8] = far[np.random.randint(len(far))]
    return np.exp2(a.ravel()).repeat(32)


def f64(x):
    return np.asarray(x).astype(np.float64)


def striped(idx):
    return np.tile(idx.reshape(-1, 16).T, (8, 1)).astype(np.uint16)


def unstriped(offs):
    return offs[:16].T.reshape(-1).astype(np.int64)


E2M1 = np.array([0.0, 0.5, 1.0, 1.5, 2.0, 3.0, 4.0, 6.0, -0.0, -0.5, -1.0, -1.5, -2.0, -3.0, -4.0, -6.0])


def pack_weight(w, fmt):
    k, n = w.shape
    w = f64(np.asarray(w, np.float32).astype(ml_dtypes.bfloat16)).reshape(k // 32, 32, n)
    amax = np.abs(w).max(1)
    if fmt == "e4m3":
        byte = np.frexp(amax)[1] - 1 + 127 - 7
    else:
        mant, ex = np.frexp(amax / 6.0)
        byte = np.where(mant > 0.5, ex, ex - 1) + 127
    byte = np.clip(np.where(amax > 0, byte, 1), 1, 254)
    scaled = (w * np.exp2(127.0 - byte)[:, None, :]).reshape(k, n).astype(np.float32)
    by_word = np.ascontiguousarray(scaled.reshape(k // 512, 128, 4, n).transpose(0, 1, 3, 2))
    if fmt == "e4m3":
        words = by_word.astype(ml_dtypes.float8_e4m3fn).view(np.uint8)
    else:
        c = by_word.astype(ml_dtypes.float4_e2m1fn).view(np.uint8) & 0xF
        words = (c[..., 0::2] | (c[..., 1::2] << 4)).reshape(k // 512, 128, 2 * n)
    return np.ascontiguousarray(words), np.ascontiguousarray(byte.astype(np.uint8).reshape(k // 512, 16, n))


def unpack_weight(words, scales, fmt):
    g, _, n = scales.shape
    words = np.ascontiguousarray(words).reshape(g, 128, n, -1)
    if fmt == "e4m3":
        vals = words.view(ml_dtypes.float8_e4m3fn).astype(np.float64)
    else:
        nib = np.empty((g, 128, n, 4), np.uint8)
        nib[..., 0::2] = words & 0xF
        nib[..., 1::2] = words >> 4
        vals = E2M1[nib]
    vals = vals * np.repeat(np.exp2(scales.astype(np.float64) - 127.0), 8, axis=1)[..., None]
    return vals.transpose(0, 1, 3, 2).reshape(g * 512, n)


def gelu(v):
    return 0.5 * v * (1.0 + np.tanh(np.sqrt(2.0 / np.pi) * (v + 0.044715 * v**3)))


K, C, H, N, T, S = 1024, 512, 1024, 512, 2048, 1024

def setup_inputs():
    n = np.random.standard_normal
    s = mx_kscale(K)[:, None]
    s2 = mx_kscale(C)[:, None]
    u = mx_kscale(H)[:, None]
    tab_words, tab_scales = pack_weight(n((K, T)) * s, "e4m3")
    tab2_words, tab2_scales = pack_weight(n((C, T)) * s2, "e4m3")
    a4_words, a4_scales = pack_weight(1.5 * n((K, H)) / np.sqrt(K) / s, "e2m1")
    w8_words, w8_scales = pack_weight(1.5 * n((H, N)) / np.sqrt(H) / u, "e4m3")
    return {
        "tab_words": tab_words, "tab_scales": tab_scales,
        "tab2_words": tab2_words, "tab2_scales": tab2_scales,
        "a4_words": a4_words, "a4_scales": a4_scales,
        "wb": (n((C, H)) / np.sqrt(C) / s2 * u.T).astype(np.float32),
        "w8_words": w8_words, "w8_scales": w8_scales,
        "gT": (0.7 * n((N, T))).astype(np.float32),
        "offs": striped(np.random.permutation(T)[:S]),
        "offs2": striped(np.random.permutation(T)[:S]),
    }

def reference(tab_words, tab_scales, tab2_words, tab2_scales, a4_words, a4_scales, wb, w8_words, w8_scales, gT, offs, offs2):
    v = unpack_weight(tab_words, tab_scales, "e4m3")[:, unstriped(offs)]
    v2 = unpack_weight(tab2_words, tab2_scales, "e4m3")[:, unstriped(offs2)]
    a4 = unpack_weight(a4_words, a4_scales, "e2m1")
    w8 = unpack_weight(w8_words, w8_scales, "e4m3")
    z = a4.T @ v
    gate = 1.0 / (1.0 + np.exp(-z))
    m = mxq(f64(wb), 0, "e4m3").T @ v2
    h = gate * m
    g = f64(gT)[:, unstriped(offs)]
    return (w8.T @ mxq(h, 0, "e4m3")) + g

@@ -1,0 +1,246 @@
+from contextlib import ExitStack
+
+import concourse.mybir as mybir
+from concourse.masks import make_identity
+
+K, C, H, N, T, S = 1024, 512, 1024, 512, 2048, 1024
+FLOPS = 2 * S * H * (K + C + N)
+
+F32 = mybir.dt.float32
+BF16 = mybir.dt.bfloat16
+I32 = mybir.dt.int32
+U32 = mybir.dt.uint32
+U16 = mybir.dt.uint16
+U8 = mybir.dt.uint8
+FP8X4 = mybir.dt.float8_e4m3fn_x4
+FP4X4 = mybir.dt.float4_e2m1fn_x4
+ACT = mybir.ActivationFunctionType
+ALU = mybir.AluOpType
+
+P = 128
+BANK = 512
+HALF = 512
+
+
+def tile_list_paged_memory_gate_kernel(
+    tc, tab_words, tab_scales, tab2_words, tab2_scales, a4_words, a4_scales, wb, w8_words, w8_scales, gT, offs, offs2, out
+):
+    nc = tc.nc
+    with ExitStack() as ctx:
+        keep = ctx.enter_context(tc.tile_pool(name="keep", bufs=1))
+        ring = ctx.enter_context(tc.tile_pool(name="ring", bufs=4))
+        psum = ctx.enter_context(tc.psum_pool(name="psum", bufs=2))
+
+        def held(shape, dtype, name):
+            return keep.tile(shape, dtype, name=name, align_bytes=64)
+
+        idx = keep.tile([P, S // 16], U16, name="idx")
+        idx2 = keep.tile([P, S // 16], U16, name="idx2")
+
+        def staged(shape, dtype, name):
+            return ring.tile(shape, dtype, name=name, tag="staged", bufs=6, align_bytes=64)
+
+        v_codes = [held([P, S], U32, f"v_codes{a}") for a in range(2)]
+        v2_codes = held([P, S], U32, "v2_codes")
+        v_scales = held([P, S], U8, "v_scales")
+        w8_planes = held([P, 2, N // 4], I32, "w8_planes")
+        v_planes = [held([P, S // 4], I32, f"v_planes{a}") for a in range(2)]
+        v2_scales = held([P, S], U8, "v2_scales")
+        a4_planes = held([P, 2, H // 4], I32, "a4_planes")
+        wb_grouped = [held([P, BANK, 4], BF16, f"wb_grouped{b}") for b in range(2)]
+        wb_codes = [held([P, BANK], U32, f"wb_codes{b}") for b in range(2)]
+        wb_planes = [held([P, BANK], U8, f"wb_planes{b}") for b in range(2)]
+        h_grouped = [[held([P, HALF, 4], BF16, f"h_grouped{b}{j}") for j in range(2)] for b in range(2)]
+        h_codes = [[held([P, HALF], U32, f"h_codes{b}{j}") for j in range(2)] for b in range(2)]
+        h_planes = [[held([P, HALF], U8, f"h_planes{b}{j}") for j in range(2)] for b in range(2)]
+        g_picked = [[held([P, HALF], F32, f"g_picked{c}{j}") for j in range(2)] for c in range(4)]
+        identity = held([P, P], F32, "identity")
+        warm = held([P, 2], F32, "warm")
+
+        def words(dram):
+            return dram.rearrange("p t i -> p (t i)").bitcast(I32)
+
+        def load_planes(queue, planes, scales):
+            for q in range(4):
+                rows = scales[:, 4 * q : 4 * q + 4, :].rearrange("a r n -> r a n")
+                queue.dma_start(planes[32 * q : 32 * q + 4, :, :], rows.bitcast(I32))
+
+        wb_rows = wb.rearrange("(p j) r -> p j r", j=4)
+        v_scale_table = staged([P, T // 4], I32, "v_scale_table")
+        v_table = [staged([P, T], I32, f"v_table{a}") for a in range(2)]
+        v2_scale_table = staged([P, T // 4], I32, "v2_scale_table")
+        a4_codes = staged([P, 2, H // 2], I32, "a4_codes")
+        nc.sync.dma_start(idx[:], offs)
+        for q in range(4):
+            nc.sync.dma_start(v_scale_table[32 * q + 24 : 32 * q + 32, :], tab_scales[:, 4 * q : 4 * q + 4, :].bitcast(I32))
+            nc.vector.memset(v_scale_table[32 * q : 32 * q + 24, :], 0)
+        for j in range(2):
+            cols = slice(j * T // 2, (j + 1) * T // 2)
+            nc.sync.dma_start(v_table[0][:, cols], words(tab_words[0])[:, cols])
+        nc.sync.dma_start(idx2[:], offs2)
+        nc.gpsimd.memset(v2_scale_table[:], 0)
+        for q in range(4):
+            nc.sync.dma_start(v2_scale_table[32 * q : 32 * q + 4, :], tab2_scales[0, 4 * q : 4 * q + 4, :].bitcast(I32))
+        wb_raw = {}
+        g_table = {}
+
+        def load_wb(b):
+            wb_raw[b] = staged([P, 4, BANK], F32, f"wb_raw{b}")
+            nc.sync.dma_start(wb_raw[b][:], wb_rows[:, :, BANK * b : BANK * (b + 1)])
+
+        def load_g(c):
+            g_table[c] = staged([P, T], F32, f"g_table{c}")
+            nc.sync.dma_start(g_table[c][:], gT[P * c : P * (c + 1), :])
+
+        load_wb(0)
+        nc.sync.dma_start(v_table[1][:], words(tab_words[1]))
+        nc.sync.dma_start(a4_codes[:], a4_words.rearrange("a p n -> p a n").bitcast(I32))
+        nc.gpsimd.memset(a4_planes[:], 0)
+        load_planes(nc.gpsimd, a4_planes, a4_scales)
+        nc.vector.memset(warm[:, 0:1], 0.0)
+        nc.scalar.activation(warm[:, 1:2], warm[:, 0:1], ACT.Sigmoid)
+        for a in range(2):
+            nc.vector.memset(v_planes[a][:], 0)
+        nc.vector.memset(w8_planes[:], 0)
+        load_planes(nc.gpsimd, w8_planes, w8_scales)
+        make_identity(nc, identity[:])
+
+        def pick(dst, table, offsets, first, count):
+            nc.vector.tensor_copy(dst, table.indirect(offsets[:, first // 16 : (first + count) // 16]))
+
+        def cast_wb(b):
+            nc.scalar.copy(
+                wb_grouped[b][:].rearrange("p (c i) t -> p c t i", i=4),
+                wb_raw[b][:].rearrange("p t (c i) -> p c t i", i=4),
+            )
+
+        def quantize(codes, planes, grouped):
+            nc.vector.quantize_mx(out=codes[:].bitcast(FP8X4), scales=planes[:], in_=grouped[:].rearrange("p n t -> p (n t)"))
+
+        gates = {}
+
+        def gate(i, b):
+            tokens = slice(P * i, P * (i + 1))
+            z = psum.tile([P, BANK], F32, name="z", tag="sums", bufs=3)
+            for a in range(2):
+                nc.tensor.matmul_mx(
+                    out=z[:],
+                    lhsT=v_codes[a][:, tokens].bitcast(FP8X4),
+                    lhsT_scale=v_planes[a][:].bitcast(U8)[:, tokens],
+                    rhs=a4_codes[:, a, :].bitcast(U8)[:, 2 * BANK * b : 2 * BANK * (b + 1)].bitcast(FP4X4),
+                    rhs_scale=a4_planes[:, a, :].bitcast(U8)[:, BANK * b : BANK * (b + 1)],
+                    start=(a == 0),
+                    stop=(a == 1),
+                )
+            sig = ring.tile([P, BANK], F32, name="sig", bufs=16)
+            nc.scalar.activation(
+                sig[:].rearrange("q (u p e) -> q u p e", u=2, e=2),
+                z[:].rearrange("q (p u e) -> q u p e", u=2, e=2),
+                ACT.Sigmoid,
+            )
+            gates[i, b] = sig
+
+        gated = {}
+
+        def gated_memory(i, b):
+            tokens = slice(P * i, P * (i + 1))
+            m = psum.tile([P, BANK], F32, name="m", bufs=3)
+            nc.tensor.matmul_mx(
+                out=m[:],
+                lhsT=v2_codes[:, tokens].bitcast(FP8X4),
+                lhsT_scale=v2_scales[:, tokens],
+                rhs=wb_codes[b][:].bitcast(FP8X4),
+                rhs_scale=wb_planes[b][:],
+                start=True,
+                stop=True,
+            )
+            h_rows = ring.tile([P, BANK], BF16, name="h_rows", bufs=16, align_bytes=64)
+            nc.vector.tensor_tensor(
+                h_rows[:].rearrange("q (u p e) -> q u p e", u=2, e=2),
+                m[:].rearrange("q (p u e) -> q u p e", u=2, e=2),
+                gates[i, b][:].rearrange("q (u p e) -> q u p e", u=2, e=2),
+                ALU.mult,
+            )
+            gated[i, b] = h_rows
+
+        def turn(pair, b):
+            turned = psum.tile([P, 2, 2, P], F32, name="turned")
+            for s in range(2):
+                pairs = gated[2 * pair + s, b][:].bitcast(F32)
+                for u in range(2):
+                    nc.tensor.transpose(turned[:, s, u, :], pairs[:, P * u : P * (u + 1)], identity[:])
+            dst = h_grouped[b][pair // 2][:].rearrange("p n t -> p (n t)").bitcast(F32)
+            dst = dst[:, BANK * (pair % 2) : BANK * (pair % 2 + 1)]
+            nc.scalar.copy(dst.rearrange("p (s r u) -> p s r u", s=2, u=2), turned[:].rearrange("p s u r -> p s r u"))
+
+        products = {}
+
+        def project(c, j, to_sbuf):
+            acc = psum.tile([P, BANK], F32, name="acc", tag="sums", bufs=3)
+            for a in (1, 0):
+                nc.tensor.matmul_mx(
+                    out=acc[:],
+                    lhsT=w8_codes[:, a, P * c : P * (c + 1)].bitcast(FP8X4),
+                    lhsT_scale=w8_planes[:, a, :].bitcast(U8)[:, P * c : P * (c + 1)],
+                    rhs=h_codes[a][j][:].bitcast(FP8X4),
+                    rhs_scale=h_planes[a][j][:],
+                    start=(a == 1),
+                    stop=(a == 0),
+                )
+            if to_sbuf:
+                y = ring.tile([P, BANK], F32, name="y", bufs=7)
+                nc.scalar.copy(y[:], acc[:])
+                products[c, j] = y
+            else:
+                products[c, j] = acc
+
+        def pick_g(c, j):
+            pick(g_picked[c][j][:], g_table[c][:], idx, HALF * j, HALF)
+
+        def finish(c, j, engine):
+            result = ring.tile([P, BANK], F32, name="result", bufs=8)
+            engine.tensor_tensor(result[:], products[c, j][:], g_picked[c][j][:], ALU.add)
+            nc.sync.dma_start(out[P * c : P * (c + 1), HALF * j : HALF * (j + 1)], result[:])
+
+        pick(v_scales[:], v_scale_table[:].bitcast(U8), idx, 0, S)
+        for a in range(2):
+            first = 24 + 4 * a
+            nc.sync.dma_start(v_planes[a][0 : P - first, :], v_scales[first:P, :].bitcast(I32))
+        v2_table = staged([P, T], I32, "v2_table")
+        nc.sync.dma_start(v2_table[:], words(tab2_words[0]))
+        pick(v_codes[0][:], v_table[0][:].bitcast(U32), idx, 0, S)
+        load_wb(1)
+        cast_wb(0)
+        load_g(0)
+        pick(v2_scales[:], v2_scale_table[:].bitcast(U8), idx2, 0, S)
+        w8_codes = staged([P, 2, N], I32, "w8_codes")
+        nc.sync.dma_start(w8_codes[:], w8_words.rearrange("a p n i -> p a (n i)").bitcast(I32))
+        for j in range(2):
+            pick(v_codes[1][:, HALF * j : HALF * (j + 1)], v_table[1][:].bitcast(U32), idx, HALF * j, HALF)
+        load_g(1)
+        quantize(wb_codes[0], wb_planes[0], wb_grouped[0])
+        for j in range(2):
+            pick(v2_codes[:, HALF * j : HALF * (j + 1)], v2_table[:].bitcast(U32), idx2, HALF * j, HALF)
+        load_g(2)
+        for i in range(8):
+            gate(i, 0)
+        cast_wb(1)
+        load_g(3)
+        quantize(wb_codes[1], wb_planes[1], wb_grouped[1])
+        for i in range(8):
+            gated_memory(i, 0)
+        for j in range(2):
+            for i in range(4 * j, 4 * j + 4):
+                gate(i, 1)
+            for i in range(4 * j, 4 * j + 4):
+                gated_memory(i, 1)
+            for b in range(2):
+                for pair in range(2 * j, 2 * j + 2):
+                    turn(pair, b)
+                quantize(h_codes[b][j], h_planes[b][j], h_grouped[b][j])
+            for c in range(4):
+                project(c, j, j == 0 or c < 2)
+        for j in range(2):
+            for c in range(4):
+                pick_g(c, j)
+                finish(c, j, nc.gpsimd if j == 0 or c < 2 else nc.vector)

@@ -38,13 +38,12 @@ def tile_list_paged_memory_gate_kernel(
         idx2 = keep.tile([P, S // 16], U16, name="idx2")
 
         def staged(shape, dtype, name):
-            return ring.tile(shape, dtype, name=name, tag="staged", bufs=6, align_bytes=64)
+            return ring.tile(shape, dtype, name=name, tag="staged", bufs=5, align_bytes=64)
 
         v_codes = [held([P, S], U32, f"v_codes{a}") for a in range(2)]
         v2_codes = held([P, S], U32, "v2_codes")
         v_scales = held([P, S], U8, "v_scales")
-        w8_planes = held([P, 2, N // 4], I32, "w8_planes")
-        v_planes = [held([P, S // 4], I32, f"v_planes{a}") for a in range(2)]
+        v_planes = held([P, 2, S // 4], I32, "v_planes")
         v2_scales = held([P, S], U8, "v2_scales")
         a4_planes = held([P, 2, H // 4], I32, "a4_planes")
         wb_grouped = [held([P, BANK, 4], BF16, f"wb_grouped{b}") for b in range(2)]
@@ -53,31 +52,33 @@ def tile_list_paged_memory_gate_kernel(
         h_grouped = [[held([P, HALF, 4], BF16, f"h_grouped{b}{j}") for j in range(2)] for b in range(2)]
         h_codes = [[held([P, HALF], U32, f"h_codes{b}{j}") for j in range(2)] for b in range(2)]
         h_planes = [[held([P, HALF], U8, f"h_planes{b}{j}") for j in range(2)] for b in range(2)]
-        g_picked = [[held([P, HALF], F32, f"g_picked{c}{j}") for j in range(2)] for c in range(4)]
+        g_picked = {(c, 0): held([P, HALF], F32, f"g_picked{c}")[:] for c in range(4)}
+        for c in range(4):
+            spent = h_grouped[c // 2][1][:].rearrange("p n t -> p (n t)").bitcast(F32)
+            g_picked[c, 1] = spent[:, HALF * (c % 2) : HALF * (c % 2 + 1)]
         identity = held([P, P], F32, "identity")
-        warm = held([P, 2], F32, "warm")
 
         def words(dram):
             return dram.rearrange("p t i -> p (t i)").bitcast(I32)
 
-        def load_planes(queue, planes, scales):
+        def load_planes(planes, scales):
             for q in range(4):
                 rows = scales[:, 4 * q : 4 * q + 4, :].rearrange("a r n -> r a n")
-                queue.dma_start(planes[32 * q : 32 * q + 4, :, :], rows.bitcast(I32))
+                nc.sync.dma_start(planes[32 * q : 32 * q + 4, :, :], rows.bitcast(I32))
 
         wb_rows = wb.rearrange("(p j) r -> p j r", j=4)
         v_scale_table = staged([P, T // 4], I32, "v_scale_table")
         v_table = [staged([P, T], I32, f"v_table{a}") for a in range(2)]
-        v2_scale_table = staged([P, T // 4], I32, "v2_scale_table")
+        v2_scale_table = keep.tile([P, T // 4], I32, name="v2_scale_table", tag="reused", align_bytes=64)
         a4_codes = staged([P, 2, H // 2], I32, "a4_codes")
-        nc.sync.dma_start(idx[:], offs)
         for q in range(4):
             nc.sync.dma_start(v_scale_table[32 * q + 24 : 32 * q + 32, :], tab_scales[:, 4 * q : 4 * q + 4, :].bitcast(I32))
             nc.vector.memset(v_scale_table[32 * q : 32 * q + 24, :], 0)
+        nc.sync.dma_start(idx[:], offs)
+        nc.sync.dma_start(idx2[:], offs2)
         for j in range(2):
             cols = slice(j * T // 2, (j + 1) * T // 2)
             nc.sync.dma_start(v_table[0][:, cols], words(tab_words[0])[:, cols])
-        nc.sync.dma_start(idx2[:], offs2)
         nc.gpsimd.memset(v2_scale_table[:], 0)
         for q in range(4):
             nc.sync.dma_start(v2_scale_table[32 * q : 32 * q + 4, :], tab2_scales[0, 4 * q : 4 * q + 4, :].bitcast(I32))
@@ -93,26 +94,27 @@ def tile_list_paged_memory_gate_kernel(
             nc.sync.dma_start(g_table[c][:], gT[P * c : P * (c + 1), :])
 
         load_wb(0)
+        nc.gpsimd.memset(a4_planes[:], 0)
+        load_planes(a4_planes, a4_scales)
         nc.sync.dma_start(v_table[1][:], words(tab_words[1]))
         nc.sync.dma_start(a4_codes[:], a4_words.rearrange("a p n -> p a n").bitcast(I32))
-        nc.gpsimd.memset(a4_planes[:], 0)
-        load_planes(nc.gpsimd, a4_planes, a4_scales)
-        nc.vector.memset(warm[:, 0:1], 0.0)
-        nc.scalar.activation(warm[:, 1:2], warm[:, 0:1], ACT.Sigmoid)
-        for a in range(2):
-            nc.vector.memset(v_planes[a][:], 0)
-        nc.vector.memset(w8_planes[:], 0)
-        load_planes(nc.gpsimd, w8_planes, w8_scales)
+        nc.vector.memset(v_planes[:], 0)
         make_identity(nc, identity[:])
 
         def pick(dst, table, offsets, first, count):
             nc.vector.tensor_copy(dst, table.indirect(offsets[:, first // 16 : (first + count) // 16]))
 
         def cast_wb(b):
-            nc.scalar.copy(
-                wb_grouped[b][:].rearrange("p (c i) t -> p c t i", i=4),
-                wb_raw[b][:].rearrange("p t (c i) -> p c t i", i=4),
-            )
+            if b == 0:
+                nc.scalar.copy(
+                    wb_grouped[b][:].rearrange("p (c i) t -> p c t i", i=2),
+                    wb_raw[b][:].rearrange("p t (c i) -> p c t i", i=2),
+                )
+            else:
+                for k in range(2):
+                    part = slice(256 * k, 256 * (k + 1))
+                    src = wb_raw[b][:].rearrange("p t n -> p n t")
+                    nc.gpsimd.tensor_scalar(wb_grouped[b][:, part, :], src[:, part, :], 1.0, 0.0, ALU.mult, ALU.add)
 
         def quantize(codes, planes, grouped):
             nc.vector.quantize_mx(out=codes[:].bitcast(FP8X4), scales=planes[:], in_=grouped[:].rearrange("p n t -> p (n t)"))
@@ -126,7 +128,7 @@ def tile_list_paged_memory_gate_kernel(
                 nc.tensor.matmul_mx(
                     out=z[:],
                     lhsT=v_codes[a][:, tokens].bitcast(FP8X4),
-                    lhsT_scale=v_planes[a][:].bitcast(U8)[:, tokens],
+                    lhsT_scale=v_planes[:, a, :].bitcast(U8)[:, tokens],
                     rhs=a4_codes[:, a, :].bitcast(U8)[:, 2 * BANK * b : 2 * BANK * (b + 1)].bitcast(FP4X4),
                     rhs_scale=a4_planes[:, a, :].bitcast(U8)[:, BANK * b : BANK * (b + 1)],
                     start=(a == 0),
@@ -195,17 +197,20 @@ def tile_list_paged_memory_gate_kernel(
                 products[c, j] = acc
 
         def pick_g(c, j):
-            pick(g_picked[c][j][:], g_table[c][:], idx, HALF * j, HALF)
+            pick(g_picked[c, j], g_table[c][:], idx, HALF * j, HALF)
 
-        def finish(c, j, engine):
+        def finish(c, j, engine, pieces=1):
             result = ring.tile([P, BANK], F32, name="result", bufs=8)
-            engine.tensor_tensor(result[:], products[c, j][:], g_picked[c][j][:], ALU.add)
-            nc.sync.dma_start(out[P * c : P * (c + 1), HALF * j : HALF * (j + 1)], result[:])
+            width = HALF // pieces
+            for first in range(0, HALF, width):
+                cols = slice(first, first + width)
+                engine.tensor_tensor(result[:, cols], products[c, j][:, cols], g_picked[c, j][:, cols], ALU.add)
+                nc.sync.dma_start(out[P * c : P * (c + 1), HALF * j + first : HALF * j + first + width], result[:, cols])
 
         pick(v_scales[:], v_scale_table[:].bitcast(U8), idx, 0, S)
         for a in range(2):
             first = 24 + 4 * a
-            nc.sync.dma_start(v_planes[a][0 : P - first, :], v_scales[first:P, :].bitcast(I32))
+            nc.sync.dma_start(v_planes[0 : P - first, a, :], v_scales[first:P, :].bitcast(I32))
         v2_table = staged([P, T], I32, "v2_table")
         nc.sync.dma_start(v2_table[:], words(tab2_words[0]))
         pick(v_codes[0][:], v_table[0][:].bitcast(U32), idx, 0, S)
@@ -213,8 +218,12 @@ def tile_list_paged_memory_gate_kernel(
         cast_wb(0)
         load_g(0)
         pick(v2_scales[:], v2_scale_table[:].bitcast(U8), idx2, 0, S)
-        w8_codes = staged([P, 2, N], I32, "w8_codes")
-        nc.sync.dma_start(w8_codes[:], w8_words.rearrange("a p n i -> p a (n i)").bitcast(I32))
+        w8_tile = keep.tile([P, 2 * N + N // 2], I32, name="w8_tile", tag="reused", align_bytes=64)
+        w8_codes = w8_tile[:, 0 : 2 * N].rearrange("p (a n) -> p a n", a=2)
+        w8_planes = w8_tile[:, 2 * N : 2 * N + N // 2].rearrange("p (a n) -> p a n", a=2)
+        nc.vector.memset(w8_planes, 0)
+        nc.sync.dma_start(w8_codes, w8_words.rearrange("a p n i -> p a (n i)").bitcast(I32))
+        load_planes(w8_planes, w8_scales)
         for j in range(2):
             pick(v_codes[1][:, HALF * j : HALF * (j + 1)], v_table[1][:].bitcast(U32), idx, HALF * j, HALF)
         load_g(1)
@@ -224,23 +233,37 @@ def tile_list_paged_memory_gate_kernel(
         load_g(2)
         for i in range(8):
             gate(i, 0)
+            gated_memory(i, 0)
         cast_wb(1)
         load_g(3)
         quantize(wb_codes[1], wb_planes[1], wb_grouped[1])
-        for i in range(8):
-            gated_memory(i, 0)
-        for j in range(2):
-            for i in range(4 * j, 4 * j + 4):
-                gate(i, 1)
-            for i in range(4 * j, 4 * j + 4):
-                gated_memory(i, 1)
-            for b in range(2):
-                for pair in range(2 * j, 2 * j + 2):
-                    turn(pair, b)
-                quantize(h_codes[b][j], h_planes[b][j], h_grouped[b][j])
-            for c in range(4):
-                project(c, j, j == 0 or c < 2)
-        for j in range(2):
-            for c in range(4):
-                pick_g(c, j)
-                finish(c, j, nc.gpsimd if j == 0 or c < 2 else nc.vector)
+        for i in range(4):
+            gate(i, 1)
+            gated_memory(i, 1)
+        for b in range(2):
+            for pair in range(2 * 0, 2 * 0 + 2):
+                turn(pair, b)
+            quantize(h_codes[b][0], h_planes[b][0], h_grouped[b][0])
+        for i in range(4, 8):
+            gate(i, 1)
+            gated_memory(i, 1)
+        for b in (0,):
+            for pair in range(2 * 1, 2 * 1 + 2):
+                turn(pair, b)
+            quantize(h_codes[b][1], h_planes[b][1], h_grouped[b][1])
+        for c in range(4):
+            project(c, 0, True)
+        for b in (1,):
+            for pair in range(2 * 1, 2 * 1 + 2):
+                turn(pair, b)
+            quantize(h_codes[b][1], h_planes[b][1], h_grouped[b][1])
+        for c in range(4):
+            pick_g(c, 0)
+        for c in range(4):
+            pick_g(c, 1)
+        for c in range(4):
+            finish(c, 0, nc.gpsimd, 1)
+        for c in range(4):
+            project(c, 1, False)
+        for c in range(4):
+            finish(c, 1, nc.vector, 2 if c == 3 else 1)

@@ -1,7 +1,6 @@
 from contextlib import ExitStack
 
 import concourse.mybir as mybir
-from concourse.masks import make_identity
 
 K, C, H, N, T, S = 1024, 512, 1024, 512, 2048, 1024
 FLOPS = 2 * S * H * (K + C + N)
@@ -20,6 +19,7 @@ ALU = mybir.AluOpType
 P = 128
 BANK = 512
 HALF = 512
+CHUNK = 256
 
 
 def tile_list_paged_memory_gate_kernel(
@@ -31,32 +31,34 @@ def tile_list_paged_memory_gate_kernel(
         ring = ctx.enter_context(tc.tile_pool(name="ring", bufs=4))
         psum = ctx.enter_context(tc.psum_pool(name="psum", bufs=2))
 
-        def held(shape, dtype, name):
-            return keep.tile(shape, dtype, name=name, align_bytes=64)
+        def held(shape, dtype, name, tag=None):
+            return keep.tile(shape, dtype, name=name, tag=tag or name, align_bytes=64)
 
         idx = keep.tile([P, S // 16], U16, name="idx")
         idx2 = keep.tile([P, S // 16], U16, name="idx2")
 
-        def staged(shape, dtype, name):
-            return ring.tile(shape, dtype, name=name, tag="staged", bufs=5, align_bytes=64)
-
+        v_scale_table = held([P, T // 4], I32, "v_scale_table")
+        v2_scale_table = held([P, T // 4], I32, "v2_scale_table")
+        v2_table = held([P, T], I32, "v2_table", "slot0")
+        wb_raw = [held([P, 4, BANK], F32, f"wb_raw{b}", f"slot{b + 1}") for b in range(2)]
+        v_table = [held([P, T], I32, "v_table0", "slot3"), held([P, T], I32, "v_table1", "slot4")]
         v_codes = [held([P, S], U32, f"v_codes{a}") for a in range(2)]
         v2_codes = held([P, S], U32, "v2_codes")
         v_scales = held([P, S], U8, "v_scales")
-        v_planes = held([P, 2, S // 4], I32, "v_planes")
+        v_moved = held([P, 2, S // 4], I32, "v_moved")
         v2_scales = held([P, S], U8, "v2_scales")
+        a4_codes = held([P, 2, H // 2], I32, "a4_codes")
         a4_planes = held([P, 2, H // 4], I32, "a4_planes")
+        a4_dealt = [held([P, 2, BANK // 2], I32, "a4_dealt0")]
+        a4_dealt_planes = [held([P, 2, BANK], U8, f"a4_dealt_planes{b}") for b in range(2)]
+        w8_codes = held([P, 2, N], I32, "w8_codes")
+        w8_planes = held([P, 2, N // 4], I32, "w8_planes")
         wb_grouped = [held([P, BANK, 4], BF16, f"wb_grouped{b}") for b in range(2)]
         wb_codes = [held([P, BANK], U32, f"wb_codes{b}") for b in range(2)]
         wb_planes = [held([P, BANK], U8, f"wb_planes{b}") for b in range(2)]
-        h_grouped = [[held([P, HALF, 4], BF16, f"h_grouped{b}{j}") for j in range(2)] for b in range(2)]
-        h_codes = [[held([P, HALF], U32, f"h_codes{b}{j}") for j in range(2)] for b in range(2)]
-        h_planes = [[held([P, HALF], U8, f"h_planes{b}{j}") for j in range(2)] for b in range(2)]
-        g_picked = {(c, 0): held([P, HALF], F32, f"g_picked{c}")[:] for c in range(4)}
-        for c in range(4):
-            spent = h_grouped[c // 2][1][:].rearrange("p n t -> p (n t)").bitcast(F32)
-            g_picked[c, 1] = spent[:, HALF * (c % 2) : HALF * (c % 2 + 1)]
-        identity = held([P, P], F32, "identity")
+        h_grouped = [held([P, 2, CHUNK, 4], BF16, f"h_grouped{k}", f"grouped{k}") for k in range(4)]
+        h_codes = [held([P, 2, CHUNK], U32, f"h_codes{k}") for k in range(4)]
+        h_planes = [held([P, 2, CHUNK], U8, f"h_planes{k}") for k in range(4)]
 
         def words(dram):
             return dram.rearrange("p t i -> p (t i)").bitcast(I32)
@@ -66,204 +68,179 @@ def tile_list_paged_memory_gate_kernel(
                 rows = scales[:, 4 * q : 4 * q + 4, :].rearrange("a r n -> r a n")
                 nc.sync.dma_start(planes[32 * q : 32 * q + 4, :, :], rows.bitcast(I32))
 
-        wb_rows = wb.rearrange("(p j) r -> p j r", j=4)
-        v_scale_table = staged([P, T // 4], I32, "v_scale_table")
-        v_table = [staged([P, T], I32, f"v_table{a}") for a in range(2)]
-        v2_scale_table = keep.tile([P, T // 4], I32, name="v2_scale_table", tag="reused", align_bytes=64)
-        a4_codes = staged([P, 2, H // 2], I32, "a4_codes")
-        for q in range(4):
-            nc.sync.dma_start(v_scale_table[32 * q + 24 : 32 * q + 32, :], tab_scales[:, 4 * q : 4 * q + 4, :].bitcast(I32))
-            nc.vector.memset(v_scale_table[32 * q : 32 * q + 24, :], 0)
-        nc.sync.dma_start(idx[:], offs)
-        nc.sync.dma_start(idx2[:], offs2)
-        for j in range(2):
-            cols = slice(j * T // 2, (j + 1) * T // 2)
-            nc.sync.dma_start(v_table[0][:, cols], words(tab_words[0])[:, cols])
-        nc.gpsimd.memset(v2_scale_table[:], 0)
-        for q in range(4):
-            nc.sync.dma_start(v2_scale_table[32 * q : 32 * q + 4, :], tab2_scales[0, 4 * q : 4 * q + 4, :].bitcast(I32))
-        wb_raw = {}
-        g_table = {}
-
-        def load_wb(b):
-            wb_raw[b] = staged([P, 4, BANK], F32, f"wb_raw{b}")
-            nc.sync.dma_start(wb_raw[b][:], wb_rows[:, :, BANK * b : BANK * (b + 1)])
-
-        def load_g(c):
-            g_table[c] = staged([P, T], F32, f"g_table{c}")
-            nc.sync.dma_start(g_table[c][:], gT[P * c : P * (c + 1), :])
-
-        load_wb(0)
-        nc.gpsimd.memset(a4_planes[:], 0)
-        load_planes(a4_planes, a4_scales)
-        nc.sync.dma_start(v_table[1][:], words(tab_words[1]))
-        nc.sync.dma_start(a4_codes[:], a4_words.rearrange("a p n -> p a n").bitcast(I32))
-        nc.vector.memset(v_planes[:], 0)
-        make_identity(nc, identity[:])
-
         def pick(dst, table, offsets, first, count):
             nc.vector.tensor_copy(dst, table.indirect(offsets[:, first // 16 : (first + count) // 16]))
 
-        def cast_wb(b):
-            if b == 0:
-                nc.scalar.copy(
-                    wb_grouped[b][:].rearrange("p (c i) t -> p c t i", i=2),
-                    wb_raw[b][:].rearrange("p t (c i) -> p c t i", i=2),
-                )
-            else:
-                for k in range(2):
-                    part = slice(256 * k, 256 * (k + 1))
-                    src = wb_raw[b][:].rearrange("p t n -> p n t")
-                    nc.gpsimd.tensor_scalar(wb_grouped[b][:, part, :], src[:, part, :], 1.0, 0.0, ALU.mult, ALU.add)
-
         def quantize(codes, planes, grouped):
-            nc.vector.quantize_mx(out=codes[:].bitcast(FP8X4), scales=planes[:], in_=grouped[:].rearrange("p n t -> p (n t)"))
+            nc.vector.quantize_mx(out=codes.bitcast(FP8X4), scales=planes, in_=grouped)
 
-        gates = {}
-
-        def gate(i, b):
-            tokens = slice(P * i, P * (i + 1))
-            z = psum.tile([P, BANK], F32, name="z", tag="sums", bufs=3)
-            for a in range(2):
-                nc.tensor.matmul_mx(
-                    out=z[:],
-                    lhsT=v_codes[a][:, tokens].bitcast(FP8X4),
-                    lhsT_scale=v_planes[:, a, :].bitcast(U8)[:, tokens],
-                    rhs=a4_codes[:, a, :].bitcast(U8)[:, 2 * BANK * b : 2 * BANK * (b + 1)].bitcast(FP4X4),
-                    rhs_scale=a4_planes[:, a, :].bitcast(U8)[:, BANK * b : BANK * (b + 1)],
-                    start=(a == 0),
-                    stop=(a == 1),
-                )
-            sig = ring.tile([P, BANK], F32, name="sig", bufs=16)
-            nc.scalar.activation(
-                sig[:].rearrange("q (u p e) -> q u p e", u=2, e=2),
-                z[:].rearrange("q (p u e) -> q u p e", u=2, e=2),
-                ACT.Sigmoid,
-            )
-            gates[i, b] = sig
-
-        gated = {}
-
-        def gated_memory(i, b):
-            tokens = slice(P * i, P * (i + 1))
-            m = psum.tile([P, BANK], F32, name="m", bufs=3)
-            nc.tensor.matmul_mx(
-                out=m[:],
-                lhsT=v2_codes[:, tokens].bitcast(FP8X4),
-                lhsT_scale=v2_scales[:, tokens],
-                rhs=wb_codes[b][:].bitcast(FP8X4),
-                rhs_scale=wb_planes[b][:],
-                start=True,
-                stop=True,
-            )
-            h_rows = ring.tile([P, BANK], BF16, name="h_rows", bufs=16, align_bytes=64)
-            nc.vector.tensor_tensor(
-                h_rows[:].rearrange("q (u p e) -> q u p e", u=2, e=2),
-                m[:].rearrange("q (p u e) -> q u p e", u=2, e=2),
-                gates[i, b][:].rearrange("q (u p e) -> q u p e", u=2, e=2),
-                ALU.mult,
-            )
-            gated[i, b] = h_rows
-
-        def turn(pair, b):
-            turned = psum.tile([P, 2, 2, P], F32, name="turned")
-            for s in range(2):
-                pairs = gated[2 * pair + s, b][:].bitcast(F32)
-                for u in range(2):
-                    nc.tensor.transpose(turned[:, s, u, :], pairs[:, P * u : P * (u + 1)], identity[:])
-            dst = h_grouped[b][pair // 2][:].rearrange("p n t -> p (n t)").bitcast(F32)
-            dst = dst[:, BANK * (pair % 2) : BANK * (pair % 2 + 1)]
-            nc.scalar.copy(dst.rearrange("p (s r u) -> p s r u", s=2, u=2), turned[:].rearrange("p s u r -> p s r u"))
-
-        products = {}
-
-        def project(c, j, to_sbuf):
-            acc = psum.tile([P, BANK], F32, name="acc", tag="sums", bufs=3)
-            for a in (1, 0):
-                nc.tensor.matmul_mx(
-                    out=acc[:],
-                    lhsT=w8_codes[:, a, P * c : P * (c + 1)].bitcast(FP8X4),
-                    lhsT_scale=w8_planes[:, a, :].bitcast(U8)[:, P * c : P * (c + 1)],
-                    rhs=h_codes[a][j][:].bitcast(FP8X4),
-                    rhs_scale=h_planes[a][j][:],
-                    start=(a == 1),
-                    stop=(a == 0),
-                )
-            if to_sbuf:
-                y = ring.tile([P, BANK], F32, name="y", bufs=7)
-                nc.scalar.copy(y[:], acc[:])
-                products[c, j] = y
+        def cast(engine, b, part):
+            dst = wb_grouped[b][:].rearrange("p (t m) j -> p m t j", t=4)[:, part]
+            src = wb_raw[b][:].rearrange("p j (m t) -> p m t j", t=4)[:, part]
+            if engine is nc.gpsimd:
+                engine.tensor_scalar(dst, src, 1.0, 0.0, ALU.mult, ALU.add)
             else:
-                products[c, j] = acc
+                engine.copy(dst, src)
 
-        def pick_g(c, j):
-            pick(g_picked[c, j], g_table[c][:], idx, HALF * j, HALF)
+        def deal(dst, src, b):
+            nc.vector.tensor_copy(
+                dst.rearrange("p a (t q) -> p a t q", t=4),
+                src[:, :, BANK * b : BANK * (b + 1)].rearrange("p a (q t) -> p a t q", t=4),
+            )
 
-        def finish(c, j, engine, pieces=1):
-            result = ring.tile([P, BANK], F32, name="result", bufs=8)
-            width = HALF // pieces
-            for first in range(0, HALF, width):
-                cols = slice(first, first + width)
-                engine.tensor_tensor(result[:, cols], products[c, j][:, cols], g_picked[c, j][:, cols], ALU.add)
-                nc.sync.dma_start(out[P * c : P * (c + 1), HALF * j + first : HALF * j + first + width], result[:, cols])
+        def deal_codes(b):
+            deal(a4_dealt[b][:].bitcast(U16), a4_codes[:].bitcast(U16), b)
 
+        def deal_planes(b):
+            deal(a4_dealt_planes[b][:], a4_planes[:].bitcast(U8), b)
+
+        wb_rows = wb.rearrange("(p j) r -> p j r", j=4)
+        out_rows = out.rearrange("(c p) s -> p c s", p=P)
+
+        for q in range(4):
+            nc.sync.dma_start(v_scale_table[32 * q + 24 : 32 * q + 32, :], tab_scales[:, 4 * q : 4 * q + 4, :].bitcast(I32))
+            nc.vector.memset(v_scale_table[32 * q : 32 * q + 24, :], 0)
+        nc.gpsimd.memset(v2_scale_table[:], 0)
+        nc.gpsimd.memset(a4_planes[:], 0)
+        nc.gpsimd.memset(v_moved[96:P, :, :], 0)
+        nc.gpsimd.memset(w8_planes[:], 0)
+        nc.sync.dma_start(idx[:], offs)
+        nc.sync.dma_start(idx2[:], offs2)
+        nc.sync.dma_start(v2_table[:], words(tab2_words[0]))
+        for q in range(4):
+            nc.sync.dma_start(v2_scale_table[32 * q : 32 * q + 4, :], tab2_scales[0, 4 * q : 4 * q + 4, :].bitcast(I32))
+        for b in range(2):
+            nc.sync.dma_start(wb_raw[b][:], wb_rows[:, :, BANK * b : BANK * (b + 1)])
+        load_planes(a4_planes, a4_scales)
+        nc.sync.dma_start(v_table[0][:], words(tab_words[0]))
+        nc.sync.dma_start(a4_codes[:], a4_words.rearrange("a p n -> p a n").bitcast(I32))
         pick(v_scales[:], v_scale_table[:].bitcast(U8), idx, 0, S)
         for a in range(2):
             first = 24 + 4 * a
-            nc.sync.dma_start(v_planes[0 : P - first, a, :], v_scales[first:P, :].bitcast(I32))
-        v2_table = staged([P, T], I32, "v2_table")
-        nc.sync.dma_start(v2_table[:], words(tab2_words[0]))
-        pick(v_codes[0][:], v_table[0][:].bitcast(U32), idx, 0, S)
-        load_wb(1)
-        cast_wb(0)
-        load_g(0)
-        pick(v2_scales[:], v2_scale_table[:].bitcast(U8), idx2, 0, S)
-        w8_tile = keep.tile([P, 2 * N + N // 2], I32, name="w8_tile", tag="reused", align_bytes=64)
-        w8_codes = w8_tile[:, 0 : 2 * N].rearrange("p (a n) -> p a n", a=2)
-        w8_planes = w8_tile[:, 2 * N : 2 * N + N // 2].rearrange("p (a n) -> p a n", a=2)
-        nc.vector.memset(w8_planes, 0)
-        nc.sync.dma_start(w8_codes, w8_words.rearrange("a p n i -> p a (n i)").bitcast(I32))
+            nc.sync.dma_start(v_moved[0 : P - first, a, :], v_scales[first:P, :].bitcast(I32))
+        v_planes = [v_moved[:, a, :].bitcast(U8) for a in range(2)]
+        nc.sync.dma_start(v_table[1][:], words(tab_words[1]))
         load_planes(w8_planes, w8_scales)
-        for j in range(2):
-            pick(v_codes[1][:, HALF * j : HALF * (j + 1)], v_table[1][:].bitcast(U32), idx, HALF * j, HALF)
-        load_g(1)
-        quantize(wb_codes[0], wb_planes[0], wb_grouped[0])
-        for j in range(2):
-            pick(v2_codes[:, HALF * j : HALF * (j + 1)], v2_table[:].bitcast(U32), idx2, HALF * j, HALF)
-        load_g(2)
-        for i in range(8):
-            gate(i, 0)
-            gated_memory(i, 0)
-        cast_wb(1)
-        load_g(3)
-        quantize(wb_codes[1], wb_planes[1], wb_grouped[1])
-        for i in range(4):
-            gate(i, 1)
-            gated_memory(i, 1)
+        nc.sync.dma_start(w8_codes[:], w8_words.rearrange("a p n i -> p a (n i)").bitcast(I32))
+
+        pick(v2_codes[:], v2_table[:].bitcast(U32), idx2, 0, S)
+        pick(v2_scales[:], v2_scale_table[:].bitcast(U8), idx2, 0, S)
         for b in range(2):
-            for pair in range(2 * 0, 2 * 0 + 2):
-                turn(pair, b)
-            quantize(h_codes[b][0], h_planes[b][0], h_grouped[b][0])
-        for i in range(4, 8):
-            gate(i, 1)
-            gated_memory(i, 1)
-        for b in (0,):
-            for pair in range(2 * 1, 2 * 1 + 2):
-                turn(pair, b)
-            quantize(h_codes[b][1], h_planes[b][1], h_grouped[b][1])
+            if b == 0:
+                cast(nc.gpsimd, b, slice(64, 128))
+                cast(nc.scalar, b, slice(0, 64))
+            else:
+                cast(nc.scalar, b, slice(0, 128))
+            quantize(wb_codes[b][:], wb_planes[b][:], wb_grouped[b][:].rearrange("p n t -> p (n t)"))
+        pick(v_codes[0][:], v_table[0][:].bitcast(U32), idx, 0, S)
+        g_table = [held([P, T], F32, f"g_table{c}", f"slot{c}") for c in range(4)]
         for c in range(4):
-            project(c, 0, True)
-        for b in (1,):
-            for pair in range(2 * 1, 2 * 1 + 2):
-                turn(pair, b)
-            quantize(h_codes[b][1], h_planes[b][1], h_grouped[b][1])
-        for c in range(4):
-            pick_g(c, 0)
-        for c in range(4):
-            pick_g(c, 1)
-        for c in range(4):
-            finish(c, 0, nc.gpsimd, 1)
-        for c in range(4):
-            project(c, 1, False)
-        for c in range(4):
-            finish(c, 1, nc.vector, 2 if c == 3 else 1)
+            nc.sync.dma_start(g_table[c][:], gT[P * c : P * (c + 1), :])
+        deal_planes(0)
+        deal_planes(1)
+        deal_codes(0)
+        pick(v_codes[1][:, 0:CHUNK], v_table[1][:].bitcast(U32), idx, 0, CHUNK)
+        pick(v_codes[1][:, CHUNK:HALF], v_table[1][:].bitcast(U32), idx, CHUNK, CHUNK)
+        pick(v_codes[1][:, HALF:S], v_table[1][:].bitcast(U32), idx, HALF, HALF)
+        a4_dealt.append(held([P, 2, BANK // 2], I32, "a4_dealt1", "slot4"))
+        deal_codes(1)
+
+        steps = [(i, b) for b in range(2) for i in range(4)] + [(2 * k + s, b) for k in (2, 3) for b in range(2) for s in range(2)]
+        on_gpsimd = (0, 1, 2, 3, 8, 9, 12, 13)
+        followed = {7: 1, 11: 1}
+
+        def memory(n, tag, bufs):
+            i, b = steps[n]
+            tokens = slice(P * i, P * (i + 1))
+            m = psum.tile([P, 4, P], F32, name="m", tag=tag, bufs=bufs)
+            for t in range(4):
+                nc.tensor.matmul_mx(
+                    out=m[:, t, :],
+                    lhsT=wb_codes[b][:, P * t : P * (t + 1)].bitcast(FP8X4),
+                    lhsT_scale=wb_planes[b][:, P * t : P * (t + 1)],
+                    rhs=v2_codes[:, tokens].bitcast(FP8X4),
+                    rhs_scale=v2_scales[:, tokens],
+                    start=True,
+                    stop=True,
+                )
+            return m[:].rearrange("p t n -> p n t")
+
+        m_rows = {}
+        for n in on_gpsimd:
+            m_rows[n] = held([P, P, 4], F32, f"m_rows{n}")
+            nc.scalar.copy(m_rows[n][:], memory(n, "sums", 5))
+
+        def gated_memory(n):
+            i, b = steps[n]
+            tokens = slice(P * i, P * (i + 1))
+            z = psum.tile([P, 4, P], F32, name="z", tag="sums", bufs=5)
+            for t in range(4):
+                for a in range(2):
+                    nc.tensor.matmul_mx(
+                        out=z[:, t, :],
+                        lhsT=a4_dealt[b][:, a, :].bitcast(U8)[:, 2 * P * t : 2 * P * (t + 1)].bitcast(FP4X4),
+                        lhsT_scale=a4_dealt_planes[b][:, a, P * t : P * (t + 1)],
+                        rhs=v_codes[a][:, tokens].bitcast(FP8X4),
+                        rhs_scale=v_planes[a][:, tokens],
+                        start=(a == 0),
+                        stop=(a == 1),
+                    )
+            if n in followed:
+                sig = held([P, P, 4], F32, f"sig{n}", f"after{n}")
+            else:
+                sig = ring.tile([P, P, 4], F32, name="sig", bufs=10)
+            nc.scalar.activation(sig[:], z[:].rearrange("p t n -> p n t"), ACT.Sigmoid)
+            h = h_grouped[i // 2][:, b, P * (i % 2) : P * (i % 2 + 1), :]
+            if n in on_gpsimd:
+                nc.gpsimd.tensor_tensor(h, m_rows[n][:], sig[:], ALU.mult)
+            else:
+                nc.vector.tensor_tensor(h, memory(n, "m", 3), sig[:], ALU.mult)
+
+        for n in range(16):
+            gated_memory(n)
+            k = steps[n][0] // 2
+            if all(i // 2 != k for i, b in steps[n + 1 :]):
+                quantize(
+                    h_codes[k][:].rearrange("p b n -> p (b n)"),
+                    h_planes[k][:].rearrange("p b n -> p (b n)"),
+                    h_grouped[k][:].rearrange("p b n t -> p (b n t)"),
+                )
+
+        groups = [held([P, 2, HALF], F32, "g_first")]
+        groups += [held([P, count, HALF], F32, f"g_after{n}", f"after{n}") for n, count in followed.items()]
+        groups += [held([P, 4, HALF], F32, "g_last", "grouped3")]
+        places = [group[:, n, :] for group in groups for n in range(group.shape[1])]
+        order = ((0, 0), (1, 0), (0, 1), (0, 2), (0, 3), (1, 1), (1, 2), (1, 3))
+        g_picked = dict(zip(order, places))
+        added_on_vector = ((1, 2), (1, 3))
+
+        def leave(j, c):
+            on_vector = (j, c) in added_on_vector
+            acc = psum.tile([P, HALF], F32, name="acc", tag="m" if on_vector else "sums", bufs=3 if on_vector else 5)
+            rows = slice(P * c, P * (c + 1))
+            for s in range(2):
+                k = 2 * j + s
+                for b in range(2):
+                    nc.tensor.matmul_mx(
+                        out=acc[:, CHUNK * s : CHUNK * (s + 1)],
+                        lhsT=w8_codes[:, b, rows].bitcast(FP8X4),
+                        lhsT_scale=w8_planes[:, b, :].bitcast(U8)[:, rows],
+                        rhs=h_codes[k][:, b, :].bitcast(FP8X4),
+                        rhs_scale=h_planes[k][:, b, :],
+                        start=(b == 0),
+                        stop=(b == 1),
+                    )
+            cols = slice(HALF * j, HALF * (j + 1))
+            result = ring.tile([P, HALF], F32, name="result", bufs=6)
+            if on_vector:
+                nc.vector.tensor_tensor(result[:], acc[:], g_picked[j, c], ALU.add)
+            else:
+                y = ring.tile([P, HALF], F32, name="y", bufs=4)
+                nc.scalar.copy(y[:], acc[:])
+                nc.gpsimd.tensor_tensor(result[:], y[:], g_picked[j, c], ALU.add)
+            nc.sync.dma_start(out[rows, cols], result[:])
+
+        for j, c in order:
+            pick(g_picked[j, c], g_table[c][:], idx, HALF * j, HALF)
+        for j, c in ((0, 0), (0, 1), (0, 2), (1, 0), (0, 3), (1, 1), (1, 2), (1, 3)):
+            leave(j, c)

@@ -37,7 +37,7 @@ def tile_list_paged_memory_gate_kernel(
         idx = keep.tile([P, S // 16], U16, name="idx")
         idx2 = keep.tile([P, S // 16], U16, name="idx2")
 
-        v_scale_table = held([P, T // 4], I32, "v_scale_table")
+        v_scale_table = held([P, T // 4], I32, "v_scale_table", "slot4")
         v2_scale_table = held([P, T // 4], I32, "v2_scale_table")
         v2_table = held([P, T], I32, "v2_table", "slot0")
         wb_raw = [held([P, 4, BANK], F32, f"wb_raw{b}", f"slot{b + 1}") for b in range(2)]
@@ -51,9 +51,7 @@ def tile_list_paged_memory_gate_kernel(
         a4_planes = held([P, 2, H // 4], I32, "a4_planes")
         a4_dealt = [held([P, 2, BANK // 2], I32, "a4_dealt0")]
         a4_dealt_planes = [held([P, 2, BANK], U8, f"a4_dealt_planes{b}") for b in range(2)]
-        w8_codes = held([P, 2, N], I32, "w8_codes")
-        w8_planes = held([P, 2, N // 4], I32, "w8_planes")
-        wb_grouped = [held([P, BANK, 4], BF16, f"wb_grouped{b}") for b in range(2)]
+        wb_grouped = [held([P, BANK, 4], BF16, f"wb_grouped{b}", f"slot{5 + b}") for b in range(2)]
         wb_codes = [held([P, BANK], U32, f"wb_codes{b}") for b in range(2)]
         wb_planes = [held([P, BANK], U8, f"wb_planes{b}") for b in range(2)]
         h_grouped = [held([P, 2, CHUNK, 4], BF16, f"h_grouped{k}", f"grouped{k}") for k in range(4)]
@@ -64,9 +62,9 @@ def tile_list_paged_memory_gate_kernel(
             return dram.rearrange("p t i -> p (t i)").bitcast(I32)
 
         def load_planes(planes, scales):
-            for q in range(4):
-                rows = scales[:, 4 * q : 4 * q + 4, :].rearrange("a r n -> r a n")
-                nc.sync.dma_start(planes[32 * q : 32 * q + 4, :, :], rows.bitcast(I32))
+            for r in range(4):
+                rows = scales[:, r:16:4, :].rearrange("a q n -> q a n")
+                nc.sync.dma_start(planes[r:P:32, :, :], rows.bitcast(I32))
 
         def pick(dst, table, offsets, first, count):
             nc.vector.tensor_copy(dst, table.indirect(offsets[:, first // 16 : (first + count) // 16]))
@@ -97,31 +95,27 @@ def tile_list_paged_memory_gate_kernel(
         wb_rows = wb.rearrange("(p j) r -> p j r", j=4)
         out_rows = out.rearrange("(c p) s -> p c s", p=P)
 
-        for q in range(4):
-            nc.sync.dma_start(v_scale_table[32 * q + 24 : 32 * q + 32, :], tab_scales[:, 4 * q : 4 * q + 4, :].bitcast(I32))
-            nc.vector.memset(v_scale_table[32 * q : 32 * q + 24, :], 0)
+        nc.sync.dma_start(v_scale_table[0:32, :], tab_scales.rearrange("a q n -> q a n").bitcast(I32))
+        nc.vector.memset(v_scale_table[32:64, :], 0)
+        nc.vector.memset(v_scale_table[64:P, :], 0)
         nc.gpsimd.memset(v2_scale_table[:], 0)
         nc.gpsimd.memset(a4_planes[:], 0)
-        nc.gpsimd.memset(v_moved[96:P, :, :], 0)
-        nc.gpsimd.memset(w8_planes[:], 0)
+        nc.gpsimd.memset(v_moved[:], 0)
         nc.sync.dma_start(idx[:], offs)
         nc.sync.dma_start(idx2[:], offs2)
         nc.sync.dma_start(v2_table[:], words(tab2_words[0]))
-        for q in range(4):
-            nc.sync.dma_start(v2_scale_table[32 * q : 32 * q + 4, :], tab2_scales[0, 4 * q : 4 * q + 4, :].bitcast(I32))
+        for r in range(4):
+            nc.sync.dma_start(v2_scale_table[r:P:32, :], tab2_scales[0, r:16:4, :].bitcast(I32))
         for b in range(2):
             nc.sync.dma_start(wb_raw[b][:], wb_rows[:, :, BANK * b : BANK * (b + 1)])
         load_planes(a4_planes, a4_scales)
         nc.sync.dma_start(v_table[0][:], words(tab_words[0]))
         nc.sync.dma_start(a4_codes[:], a4_words.rearrange("a p n -> p a n").bitcast(I32))
         pick(v_scales[:], v_scale_table[:].bitcast(U8), idx, 0, S)
-        for a in range(2):
-            first = 24 + 4 * a
-            nc.sync.dma_start(v_moved[0 : P - first, a, :], v_scales[first:P, :].bitcast(I32))
+        for q in range(4):
+            nc.sync.dma_start(v_moved[32 * q : 32 * q + 4, :, :], v_scales[8 * q : 8 * q + 8, :].bitcast(I32))
         v_planes = [v_moved[:, a, :].bitcast(U8) for a in range(2)]
         nc.sync.dma_start(v_table[1][:], words(tab_words[1]))
-        load_planes(w8_planes, w8_scales)
-        nc.sync.dma_start(w8_codes[:], w8_words.rearrange("a p n i -> p a (n i)").bitcast(I32))
 
         pick(v2_codes[:], v2_table[:].bitcast(U32), idx2, 0, S)
         pick(v2_scales[:], v2_scale_table[:].bitcast(U8), idx2, 0, S)
@@ -132,10 +126,17 @@ def tile_list_paged_memory_gate_kernel(
             else:
                 cast(nc.scalar, b, slice(0, 128))
             quantize(wb_codes[b][:], wb_planes[b][:], wb_grouped[b][:].rearrange("p n t -> p (n t)"))
+        w8_tile = held([P, 2 * N + N // 2], I32, "w8_tile", "slot5")
+        w8_codes = w8_tile[:, 0 : 2 * N].rearrange("p (a n) -> p a n", a=2)
+        w8_planes = w8_tile[:, 2 * N : 2 * N + N // 2].rearrange("p (a n) -> p a n", a=2)
+        nc.gpsimd.memset(w8_planes, 0)
+        nc.sync.dma_start(w8_codes, w8_words.rearrange("a p n i -> p a (n i)").bitcast(I32))
         pick(v_codes[0][:], v_table[0][:].bitcast(U32), idx, 0, S)
         g_table = [held([P, T], F32, f"g_table{c}", f"slot{c}") for c in range(4)]
         for c in range(4):
             nc.sync.dma_start(g_table[c][:], gT[P * c : P * (c + 1), :])
+            if c == 1:
+                load_planes(w8_planes, w8_scales)
         deal_planes(0)
         deal_planes(1)
         deal_codes(0)

@@ -37,19 +37,19 @@ def tile_list_paged_memory_gate_kernel(
         idx = keep.tile([P, S // 16], U16, name="idx")
         idx2 = keep.tile([P, S // 16], U16, name="idx2")
 
-        v_scale_table = held([P, T // 4], I32, "v_scale_table", "slot4")
+        v_scale_table = held([P, T // 4], I32, "v_scale_table")
         v2_scale_table = held([P, T // 4], I32, "v2_scale_table")
         v2_table = held([P, T], I32, "v2_table", "slot0")
         wb_raw = [held([P, 4, BANK], F32, f"wb_raw{b}", f"slot{b + 1}") for b in range(2)]
         v_table = [held([P, T], I32, "v_table0", "slot3"), held([P, T], I32, "v_table1", "slot4")]
-        v_codes = [held([P, S], U32, f"v_codes{a}") for a in range(2)]
+        v_codes = {(a, j): held([P, HALF], U32, f"v_codes{a}{j}", "slot7" if (a, j) == (0, 1) else None) for a in range(2) for j in range(2)}
         v2_codes = held([P, S], U32, "v2_codes")
-        v_scales = held([P, S], U8, "v_scales")
+        v_scales = held([P, S], U8, "v_scales", "slot7")
         v_moved = held([P, 2, S // 4], I32, "v_moved")
         v2_scales = held([P, S], U8, "v2_scales")
         a4_codes = held([P, 2, H // 2], I32, "a4_codes")
         a4_planes = held([P, 2, H // 4], I32, "a4_planes")
-        a4_dealt = [held([P, 2, BANK // 2], I32, "a4_dealt0")]
+        a4_dealt = [held([P, 2, BANK // 2], I32, f"a4_dealt{b}") for b in range(2)]
         a4_dealt_planes = [held([P, 2, BANK], U8, f"a4_dealt_planes{b}") for b in range(2)]
         wb_grouped = [held([P, BANK, 4], BF16, f"wb_grouped{b}", f"slot{5 + b}") for b in range(2)]
         wb_codes = [held([P, BANK], U32, f"wb_codes{b}") for b in range(2)]
@@ -80,17 +80,18 @@ def tile_list_paged_memory_gate_kernel(
             else:
                 engine.copy(dst, src)
 
-        def deal(dst, src, b):
-            nc.vector.tensor_copy(
+        def deal(engine, dst, src, b):
+            engine.tensor_copy(
                 dst.rearrange("p a (t q) -> p a t q", t=4),
                 src[:, :, BANK * b : BANK * (b + 1)].rearrange("p a (q t) -> p a t q", t=4),
             )
 
         def deal_codes(b):
-            deal(a4_dealt[b][:].bitcast(U16), a4_codes[:].bitcast(U16), b)
+            deal(nc.vector, a4_dealt[b][:].bitcast(U16), a4_codes[:].bitcast(U16), b)
 
         def deal_planes(b):
-            deal(a4_dealt_planes[b][:], a4_planes[:].bitcast(U8), b)
+            for a in range(2):
+                deal(nc.gpsimd, a4_dealt_planes[b][:, a : a + 1, :], a4_planes[:, a : a + 1, :].bitcast(U8), b)
 
         wb_rows = wb.rearrange("(p j) r -> p j r", j=4)
         out_rows = out.rearrange("(c p) s -> p c s", p=P)
@@ -106,49 +107,46 @@ def tile_list_paged_memory_gate_kernel(
         nc.sync.dma_start(v2_table[:], words(tab2_words[0]))
         for r in range(4):
             nc.sync.dma_start(v2_scale_table[r:P:32, :], tab2_scales[0, r:16:4, :].bitcast(I32))
-        for b in range(2):
-            nc.sync.dma_start(wb_raw[b][:], wb_rows[:, :, BANK * b : BANK * (b + 1)])
+        nc.sync.dma_start(wb_raw[0][:], wb_rows[:, :, 0:BANK])
         load_planes(a4_planes, a4_scales)
+        nc.sync.dma_start(wb_raw[1][:], wb_rows[:, :, BANK : 2 * BANK])
         nc.sync.dma_start(v_table[0][:], words(tab_words[0]))
         nc.sync.dma_start(a4_codes[:], a4_words.rearrange("a p n -> p a n").bitcast(I32))
+        nc.sync.dma_start(v_table[1][:], words(tab_words[1]))
         pick(v_scales[:], v_scale_table[:].bitcast(U8), idx, 0, S)
         for q in range(4):
             nc.sync.dma_start(v_moved[32 * q : 32 * q + 4, :, :], v_scales[8 * q : 8 * q + 8, :].bitcast(I32))
         v_planes = [v_moved[:, a, :].bitcast(U8) for a in range(2)]
-        nc.sync.dma_start(v_table[1][:], words(tab_words[1]))
 
         pick(v2_codes[:], v2_table[:].bitcast(U32), idx2, 0, S)
         pick(v2_scales[:], v2_scale_table[:].bitcast(U8), idx2, 0, S)
         for b in range(2):
-            if b == 0:
-                cast(nc.gpsimd, b, slice(64, 128))
-                cast(nc.scalar, b, slice(0, 64))
-            else:
-                cast(nc.scalar, b, slice(0, 128))
+            cast(nc.scalar, b, slice(0, 128))
             quantize(wb_codes[b][:], wb_planes[b][:], wb_grouped[b][:].rearrange("p n t -> p (n t)"))
         w8_tile = held([P, 2 * N + N // 2], I32, "w8_tile", "slot5")
         w8_codes = w8_tile[:, 0 : 2 * N].rearrange("p (a n) -> p a n", a=2)
         w8_planes = w8_tile[:, 2 * N : 2 * N + N // 2].rearrange("p (a n) -> p a n", a=2)
         nc.gpsimd.memset(w8_planes, 0)
         nc.sync.dma_start(w8_codes, w8_words.rearrange("a p n i -> p a (n i)").bitcast(I32))
-        pick(v_codes[0][:], v_table[0][:].bitcast(U32), idx, 0, S)
+        pick(v_codes[0, 0][:], v_table[0][:].bitcast(U32), idx, 0, HALF)
         g_table = [held([P, T], F32, f"g_table{c}", f"slot{c}") for c in range(4)]
-        for c in range(4):
+        for c in range(3):
             nc.sync.dma_start(g_table[c][:], gT[P * c : P * (c + 1), :])
             if c == 1:
                 load_planes(w8_planes, w8_scales)
         deal_planes(0)
         deal_planes(1)
         deal_codes(0)
-        pick(v_codes[1][:, 0:CHUNK], v_table[1][:].bitcast(U32), idx, 0, CHUNK)
-        pick(v_codes[1][:, CHUNK:HALF], v_table[1][:].bitcast(U32), idx, CHUNK, CHUNK)
-        pick(v_codes[1][:, HALF:S], v_table[1][:].bitcast(U32), idx, HALF, HALF)
-        a4_dealt.append(held([P, 2, BANK // 2], I32, "a4_dealt1", "slot4"))
         deal_codes(1)
+        for first in (0, CHUNK):
+            pick(v_codes[1, 0][:, first : first + CHUNK], v_table[1][:].bitcast(U32), idx, first, CHUNK)
+        for a in range(2):
+            pick(v_codes[a, 1][:], v_table[a][:].bitcast(U32), idx, HALF, HALF)
+        nc.sync.dma_start(g_table[3][:], gT[3 * P : 4 * P, :])
 
         steps = [(i, b) for b in range(2) for i in range(4)] + [(2 * k + s, b) for k in (2, 3) for b in range(2) for s in range(2)]
         on_gpsimd = (0, 1, 2, 3, 8, 9, 12, 13)
-        followed = {7: 1, 11: 1}
+        followed = {5: 1, 7: 1, 11: 1}
 
         def memory(n, tag, bufs):
             i, b = steps[n]
@@ -181,7 +179,7 @@ def tile_list_paged_memory_gate_kernel(
                         out=z[:, t, :],
                         lhsT=a4_dealt[b][:, a, :].bitcast(U8)[:, 2 * P * t : 2 * P * (t + 1)].bitcast(FP4X4),
                         lhsT_scale=a4_dealt_planes[b][:, a, P * t : P * (t + 1)],
-                        rhs=v_codes[a][:, tokens].bitcast(FP8X4),
+                        rhs=v_codes[a, i // 4][:, P * (i % 4) : P * (i % 4 + 1)].bitcast(FP8X4),
                         rhs_scale=v_planes[a][:, tokens],
                         start=(a == 0),
                         stop=(a == 1),
@@ -209,11 +207,11 @@ def tile_list_paged_memory_gate_kernel(
 
         groups = [held([P, 2, HALF], F32, "g_first")]
         groups += [held([P, count, HALF], F32, f"g_after{n}", f"after{n}") for n, count in followed.items()]
-        groups += [held([P, 4, HALF], F32, "g_last", "grouped3")]
+        groups += [held([P, 3, HALF], F32, "g_last", "grouped3")]
         places = [group[:, n, :] for group in groups for n in range(group.shape[1])]
         order = ((0, 0), (1, 0), (0, 1), (0, 2), (0, 3), (1, 1), (1, 2), (1, 3))
         g_picked = dict(zip(order, places))
-        added_on_vector = ((1, 2), (1, 3))
+        added_on_vector = ((1, 1), (1, 2), (1, 3))
 
         def leave(j, c):
             on_vector = (j, c) in added_on_vector
@@ -234,14 +232,21 @@ def tile_list_paged_memory_gate_kernel(
             cols = slice(HALF * j, HALF * (j + 1))
             result = ring.tile([P, HALF], F32, name="result", bufs=6)
             if on_vector:
-                nc.vector.tensor_tensor(result[:], acc[:], g_picked[j, c], ALU.add)
+                width = CHUNK if (j, c) == order[-1] else HALF
+                for first in range(0, HALF, width):
+                    part = slice(first, first + width)
+                    nc.vector.tensor_tensor(result[:, part], acc[:, part], g_picked[j, c][:, part], ALU.add)
+                    nc.sync.dma_start(out[rows, cols][:, part], result[:, part])
             else:
                 y = ring.tile([P, HALF], F32, name="y", bufs=4)
                 nc.scalar.copy(y[:], acc[:])
                 nc.gpsimd.tensor_tensor(result[:], y[:], g_picked[j, c], ALU.add)
-            nc.sync.dma_start(out[rows, cols], result[:])
+                nc.sync.dma_start(out[rows, cols], result[:])
 
-        for j, c in order:
+        for n, (j, c) in enumerate(order):
             pick(g_picked[j, c], g_table[c][:], idx, HALF * j, HALF)
-        for j, c in ((0, 0), (0, 1), (0, 2), (1, 0), (0, 3), (1, 1), (1, 2), (1, 3)):
-            leave(j, c)
+            if n >= 5:
+                leave(j, c)
+            elif n == 4:
+                for j, c in ((0, 0), (0, 1), (0, 2), (1, 0), (0, 3)):
+                    leave(j, c)

@@ -42,7 +42,7 @@ def tile_list_paged_memory_gate_kernel(
         v2_table = held([P, T], I32, "v2_table", "slot0")
         wb_raw = [held([P, 4, BANK], F32, f"wb_raw{b}", f"slot{b + 1}") for b in range(2)]
         v_table = [held([P, T], I32, "v_table0", "slot3"), held([P, T], I32, "v_table1", "slot4")]
-        v_codes = {(a, j): held([P, HALF], U32, f"v_codes{a}{j}", "slot7" if (a, j) == (0, 1) else None) for a in range(2) for j in range(2)}
+        v_codes = {(a, j): held([P, HALF], U32, f"v_codes{a}{j}", None) for a in range(2) for j in range(2)}
         v2_codes = held([P, S], U32, "v2_codes")
         v_scales = held([P, S], U8, "v_scales", "slot7")
         v_moved = held([P, 2, S // 4], I32, "v_moved")
@@ -80,18 +80,18 @@ def tile_list_paged_memory_gate_kernel(
             else:
                 engine.copy(dst, src)
 
-        def deal(engine, dst, src, b):
-            engine.tensor_copy(
-                dst.rearrange("p a (t q) -> p a t q", t=4),
-                src[:, :, BANK * b : BANK * (b + 1)].rearrange("p a (q t) -> p a t q", t=4),
-            )
+        def deal(dst, src, b, width):
+            for a in range(2):
+                nc.gpsimd.tensor_copy(
+                    dst[:, a, :].rearrange("p (t q e) -> p t q e", t=4, e=width),
+                    src[:, a, width * BANK * b : width * BANK * (b + 1)].rearrange("p (q t e) -> p t q e", t=4, e=width),
+                )
 
         def deal_codes(b):
-            deal(nc.vector, a4_dealt[b][:].bitcast(U16), a4_codes[:].bitcast(U16), b)
+            deal(a4_dealt[b][:].bitcast(U8), a4_codes[:].bitcast(U8), b, 2)
 
         def deal_planes(b):
-            for a in range(2):
-                deal(nc.gpsimd, a4_dealt_planes[b][:, a : a + 1, :], a4_planes[:, a : a + 1, :].bitcast(U8), b)
+            deal(a4_dealt_planes[b][:], a4_planes[:].bitcast(U8), b, 1)
 
         wb_rows = wb.rearrange("(p j) r -> p j r", j=4)
         out_rows = out.rearrange("(c p) s -> p c s", p=P)
@@ -110,8 +110,8 @@ def tile_list_paged_memory_gate_kernel(
         nc.sync.dma_start(wb_raw[0][:], wb_rows[:, :, 0:BANK])
         load_planes(a4_planes, a4_scales)
         nc.sync.dma_start(wb_raw[1][:], wb_rows[:, :, BANK : 2 * BANK])
-        nc.sync.dma_start(v_table[0][:], words(tab_words[0]))
         nc.sync.dma_start(a4_codes[:], a4_words.rearrange("a p n -> p a n").bitcast(I32))
+        nc.sync.dma_start(v_table[0][:], words(tab_words[0]))
         nc.sync.dma_start(v_table[1][:], words(tab_words[1]))
         pick(v_scales[:], v_scale_table[:].bitcast(U8), idx, 0, S)
         for q in range(4):
@@ -128,7 +128,8 @@ def tile_list_paged_memory_gate_kernel(
         w8_planes = w8_tile[:, 2 * N : 2 * N + N // 2].rearrange("p (a n) -> p a n", a=2)
         nc.gpsimd.memset(w8_planes, 0)
         nc.sync.dma_start(w8_codes, w8_words.rearrange("a p n i -> p a (n i)").bitcast(I32))
-        pick(v_codes[0, 0][:], v_table[0][:].bitcast(U32), idx, 0, HALF)
+        for j in range(2):
+            pick(v_codes[0, j][:], v_table[0][:].bitcast(U32), idx, HALF * j, HALF)
         g_table = [held([P, T], F32, f"g_table{c}", f"slot{c}") for c in range(4)]
         for c in range(3):
             nc.sync.dma_start(g_table[c][:], gT[P * c : P * (c + 1), :])
@@ -140,8 +141,7 @@ def tile_list_paged_memory_gate_kernel(
         deal_codes(1)
         for first in (0, CHUNK):
             pick(v_codes[1, 0][:, first : first + CHUNK], v_table[1][:].bitcast(U32), idx, first, CHUNK)
-        for a in range(2):
-            pick(v_codes[a, 1][:], v_table[a][:].bitcast(U32), idx, HALF, HALF)
+        pick(v_codes[1, 1][:], v_table[1][:].bitcast(U32), idx, HALF, HALF)
         nc.sync.dma_start(g_table[3][:], gT[3 * P : 4 * P, :])
 
         steps = [(i, b) for b in range(2) for i in range(4)] + [(2 * k + s, b) for k in (2, 3) for b in range(2) for s in range(2)]

@@ -42,21 +42,27 @@ def tile_list_paged_memory_gate_kernel(
         v2_table = held([P, T], I32, "v2_table", "slot0")
         wb_raw = [held([P, 4, BANK], F32, f"wb_raw{b}", f"slot{b + 1}") for b in range(2)]
         v_table = [held([P, T], I32, "v_table0", "slot3"), held([P, T], I32, "v_table1", "slot4")]
-        v_codes = {(a, j): held([P, HALF], U32, f"v_codes{a}{j}", None) for a in range(2) for j in range(2)}
+        v_codes = [held([P, S], U32, f"v_codes{a}") for a in range(2)]
         v2_codes = held([P, S], U32, "v2_codes")
         v_scales = held([P, S], U8, "v_scales", "slot7")
         v_moved = held([P, 2, S // 4], I32, "v_moved")
         v2_scales = held([P, S], U8, "v2_scales")
         a4_codes = held([P, 2, H // 2], I32, "a4_codes")
         a4_planes = held([P, 2, H // 4], I32, "a4_planes")
-        a4_dealt = [held([P, 2, BANK // 2], I32, f"a4_dealt{b}") for b in range(2)]
+        a4_dealt = held([P, 2, H // 2], I32, "a4_dealt")
         a4_dealt_planes = [held([P, 2, BANK], U8, f"a4_dealt_planes{b}") for b in range(2)]
         wb_grouped = [held([P, BANK, 4], BF16, f"wb_grouped{b}", f"slot{5 + b}") for b in range(2)]
         wb_codes = [held([P, BANK], U32, f"wb_codes{b}") for b in range(2)]
         wb_planes = [held([P, BANK], U8, f"wb_planes{b}") for b in range(2)]
-        h_grouped = [held([P, 2, CHUNK, 4], BF16, f"h_grouped{k}", f"grouped{k}") for k in range(4)]
-        h_codes = [held([P, 2, CHUNK], U32, f"h_codes{k}") for k in range(4)]
-        h_planes = [held([P, 2, CHUNK], U8, f"h_planes{k}") for k in range(4)]
+        runs = ((0, 2), (2, 1), (3, 1))
+        h_runs, h_grouped, h_codes, h_planes = {}, {}, {}, {}
+        for first, count in runs:
+            grouped = held([P, count, 2, CHUNK, 4], BF16, f"h_grouped{first}", f"grouped{first}")
+            codes = held([P, count, 2, CHUNK], U32, f"h_codes{first}")
+            planes = held([P, count, 2, CHUNK], U8, f"h_planes{first}")
+            h_runs[first + count - 1] = (codes, planes, grouped)
+            for k in range(count):
+                h_grouped[first + k], h_codes[first + k], h_planes[first + k] = grouped[:, k], codes[:, k], planes[:, k]
 
         def words(dram):
             return dram.rearrange("p t i -> p (t i)").bitcast(I32)
@@ -87,8 +93,11 @@ def tile_list_paged_memory_gate_kernel(
                     src[:, a, width * BANK * b : width * BANK * (b + 1)].rearrange("p (q t e) -> p t q e", t=4, e=width),
                 )
 
-        def deal_codes(b):
-            deal(a4_dealt[b][:].bitcast(U8), a4_codes[:].bitcast(U8), b, 2)
+        def deal_codes():
+            nc.vector.tensor_copy(
+                a4_dealt[:].bitcast(U16).rearrange("p a (b t q) -> p (a b) t q", b=2, t=4),
+                a4_codes[:].bitcast(U16).rearrange("p a (b q t) -> p (a b) t q", b=2, t=4),
+            )
 
         def deal_planes(b):
             deal(a4_dealt_planes[b][:], a4_planes[:].bitcast(U8), b, 1)
@@ -128,8 +137,7 @@ def tile_list_paged_memory_gate_kernel(
         w8_planes = w8_tile[:, 2 * N : 2 * N + N // 2].rearrange("p (a n) -> p a n", a=2)
         nc.gpsimd.memset(w8_planes, 0)
         nc.sync.dma_start(w8_codes, w8_words.rearrange("a p n i -> p a (n i)").bitcast(I32))
-        for j in range(2):
-            pick(v_codes[0, j][:], v_table[0][:].bitcast(U32), idx, HALF * j, HALF)
+        pick(v_codes[0][:], v_table[0][:].bitcast(U32), idx, 0, S)
         g_table = [held([P, T], F32, f"g_table{c}", f"slot{c}") for c in range(4)]
         for c in range(3):
             nc.sync.dma_start(g_table[c][:], gT[P * c : P * (c + 1), :])
@@ -137,11 +145,9 @@ def tile_list_paged_memory_gate_kernel(
                 load_planes(w8_planes, w8_scales)
         deal_planes(0)
         deal_planes(1)
-        deal_codes(0)
-        deal_codes(1)
-        for first in (0, CHUNK):
-            pick(v_codes[1, 0][:, first : first + CHUNK], v_table[1][:].bitcast(U32), idx, first, CHUNK)
-        pick(v_codes[1, 1][:], v_table[1][:].bitcast(U32), idx, HALF, HALF)
+        deal_codes()
+        for first, count in ((0, CHUNK), (CHUNK, CHUNK), (HALF, HALF)):
+            pick(v_codes[1][:, first : first + count], v_table[1][:].bitcast(U32), idx, first, count)
         nc.sync.dma_start(g_table[3][:], gT[3 * P : 4 * P, :])
 
         steps = [(i, b) for b in range(2) for i in range(4)] + [(2 * k + s, b) for k in (2, 3) for b in range(2) for s in range(2)]
@@ -177,9 +183,9 @@ def tile_list_paged_memory_gate_kernel(
                 for a in range(2):
                     nc.tensor.matmul_mx(
                         out=z[:, t, :],
-                        lhsT=a4_dealt[b][:, a, :].bitcast(U8)[:, 2 * P * t : 2 * P * (t + 1)].bitcast(FP4X4),
+                        lhsT=a4_dealt[:, a, :].bitcast(U8)[:, 2 * (BANK * b + P * t) : 2 * (BANK * b + P * (t + 1))].bitcast(FP4X4),
                         lhsT_scale=a4_dealt_planes[b][:, a, P * t : P * (t + 1)],
-                        rhs=v_codes[a, i // 4][:, P * (i % 4) : P * (i % 4 + 1)].bitcast(FP8X4),
+                        rhs=v_codes[a][:, tokens].bitcast(FP8X4),
                         rhs_scale=v_planes[a][:, tokens],
                         start=(a == 0),
                         stop=(a == 1),
@@ -199,11 +205,13 @@ def tile_list_paged_memory_gate_kernel(
             gated_memory(n)
             k = steps[n][0] // 2
             if all(i // 2 != k for i, b in steps[n + 1 :]):
-                quantize(
-                    h_codes[k][:].rearrange("p b n -> p (b n)"),
-                    h_planes[k][:].rearrange("p b n -> p (b n)"),
-                    h_grouped[k][:].rearrange("p b n t -> p (b n t)"),
-                )
+                if k in h_runs:
+                    codes, planes, grouped = h_runs[k]
+                    quantize(
+                        codes[:].rearrange("p k b n -> p (k b n)"),
+                        planes[:].rearrange("p k b n -> p (k b n)"),
+                        grouped[:].rearrange("p k b n t -> p (k b n t)"),
+                    )
 
         groups = [held([P, 2, HALF], F32, "g_first")]
         groups += [held([P, count, HALF], F32, f"g_after{n}", f"after{n}") for n, count in followed.items()]
@@ -243,8 +251,10 @@ def tile_list_paged_memory_gate_kernel(
                 nc.gpsimd.tensor_tensor(result[:], y[:], g_picked[j, c], ALU.add)
                 nc.sync.dma_start(out[rows, cols], result[:])
 
+        pick(groups[0][:].rearrange("p j n -> p (j n)"), g_table[0][:], idx, 0, S)
         for n, (j, c) in enumerate(order):
-            pick(g_picked[j, c], g_table[c][:], idx, HALF * j, HALF)
+            if c > 0:
+                pick(g_picked[j, c], g_table[c][:], idx, HALF * j, HALF)
             if n >= 5:
                 leave(j, c)
             elif n == 4:

@@ -213,11 +213,11 @@ def tile_list_paged_memory_gate_kernel(
                         grouped[:].rearrange("p k b n t -> p (k b n t)"),
                     )
 
-        groups = [held([P, 2, HALF], F32, "g_first")]
+        groups = [held([P, 3, HALF], F32, "g_first")]
         groups += [held([P, count, HALF], F32, f"g_after{n}", f"after{n}") for n, count in followed.items()]
-        groups += [held([P, 3, HALF], F32, "g_last", "grouped3")]
+        groups += [held([P, 1, HALF], F32, "g_last0", "grouped3"), held([P, 1, HALF], F32, "g_last1", "after5")]
         places = [group[:, n, :] for group in groups for n in range(group.shape[1])]
-        order = ((0, 0), (1, 0), (0, 1), (0, 2), (0, 3), (1, 1), (1, 2), (1, 3))
+        order = ((0, 0), (1, 0), (0, 1), (1, 1), (0, 2), (0, 3), (1, 2), (1, 3))
         g_picked = dict(zip(order, places))
         added_on_vector = ((1, 1), (1, 2), (1, 3))
 
@@ -251,12 +251,10 @@ def tile_list_paged_memory_gate_kernel(
                 nc.gpsimd.tensor_tensor(result[:], y[:], g_picked[j, c], ALU.add)
                 nc.sync.dma_start(out[rows, cols], result[:])
 
-        pick(groups[0][:].rearrange("p j n -> p (j n)"), g_table[0][:], idx, 0, S)
-        for n, (j, c) in enumerate(order):
-            if c > 0:
+        pick(groups[0][:, 0:2, :].rearrange("p j n -> p (j n)"), g_table[0][:], idx, 0, S)
+        for j, c in order[2:-1]:
+            pick(g_picked[j, c], g_table[c][:], idx, HALF * j, HALF)
+        for j, c in ((0, 0), (0, 1), (0, 2), (0, 3), (1, 1), (1, 0), (1, 2), (1, 3)):
+            if (j, c) == order[-1]:
                 pick(g_picked[j, c], g_table[c][:], idx, HALF * j, HALF)
-            if n >= 5:
-                leave(j, c)
-            elif n == 4:
-                for j, c in ((0, 0), (0, 1), (0, 2), (1, 0), (0, 3)):
-                    leave(j, c)
+            leave(j, c)

@@ -19,7 +19,6 @@ ALU = mybir.AluOpType
 P = 128
 BANK = 512
 HALF = 512
-CHUNK = 256
 
 
 def tile_list_paged_memory_gate_kernel(
@@ -29,40 +28,10 @@ def tile_list_paged_memory_gate_kernel(
     with ExitStack() as ctx:
         keep = ctx.enter_context(tc.tile_pool(name="keep", bufs=1))
         ring = ctx.enter_context(tc.tile_pool(name="ring", bufs=4))
-        psum = ctx.enter_context(tc.psum_pool(name="psum", bufs=2))
+        psum = ctx.enter_context(tc.psum_pool(name="psum", bufs=4))
 
         def held(shape, dtype, name, tag=None):
             return keep.tile(shape, dtype, name=name, tag=tag or name, align_bytes=64)
-
-        idx = keep.tile([P, S // 16], U16, name="idx")
-        idx2 = keep.tile([P, S // 16], U16, name="idx2")
-
-        v_scale_table = held([P, T // 4], I32, "v_scale_table")
-        v2_scale_table = held([P, T // 4], I32, "v2_scale_table")
-        v2_table = held([P, T], I32, "v2_table", "slot0")
-        wb_raw = [held([P, 4, BANK], F32, f"wb_raw{b}", f"slot{b + 1}") for b in range(2)]
-        v_table = [held([P, T], I32, "v_table0", "slot3"), held([P, T], I32, "v_table1", "slot4")]
-        v_codes = [held([P, S], U32, f"v_codes{a}") for a in range(2)]
-        v2_codes = held([P, S], U32, "v2_codes")
-        v_scales = held([P, S], U8, "v_scales", "slot7")
-        v_moved = held([P, 2, S // 4], I32, "v_moved")
-        v2_scales = held([P, S], U8, "v2_scales")
-        a4_codes = held([P, 2, H // 2], I32, "a4_codes")
-        a4_planes = held([P, 2, H // 4], I32, "a4_planes")
-        a4_dealt = held([P, 2, H // 2], I32, "a4_dealt")
-        a4_dealt_planes = [held([P, 2, BANK], U8, f"a4_dealt_planes{b}") for b in range(2)]
-        wb_grouped = [held([P, BANK, 4], BF16, f"wb_grouped{b}", f"slot{5 + b}") for b in range(2)]
-        wb_codes = [held([P, BANK], U32, f"wb_codes{b}") for b in range(2)]
-        wb_planes = [held([P, BANK], U8, f"wb_planes{b}") for b in range(2)]
-        runs = ((0, 2), (2, 1), (3, 1))
-        h_runs, h_grouped, h_codes, h_planes = {}, {}, {}, {}
-        for first, count in runs:
-            grouped = held([P, count, 2, CHUNK, 4], BF16, f"h_grouped{first}", f"grouped{first}")
-            codes = held([P, count, 2, CHUNK], U32, f"h_codes{first}")
-            planes = held([P, count, 2, CHUNK], U8, f"h_planes{first}")
-            h_runs[first + count - 1] = (codes, planes, grouped)
-            for k in range(count):
-                h_grouped[first + k], h_codes[first + k], h_planes[first + k] = grouped[:, k], codes[:, k], planes[:, k]
 
         def words(dram):
             return dram.rearrange("p t i -> p (t i)").bitcast(I32)
@@ -78,183 +47,203 @@ def tile_list_paged_memory_gate_kernel(
         def quantize(codes, planes, grouped):
             nc.vector.quantize_mx(out=codes.bitcast(FP8X4), scales=planes, in_=grouped)
 
-        def cast(engine, b, part):
-            dst = wb_grouped[b][:].rearrange("p (t m) j -> p m t j", t=4)[:, part]
-            src = wb_raw[b][:].rearrange("p j (m t) -> p m t j", t=4)[:, part]
-            if engine is nc.gpsimd:
-                engine.tensor_scalar(dst, src, 1.0, 0.0, ALU.mult, ALU.add)
-            else:
-                engine.copy(dst, src)
-
-        def deal(dst, src, b, width):
-            for a in range(2):
-                nc.gpsimd.tensor_copy(
-                    dst[:, a, :].rearrange("p (t q e) -> p t q e", t=4, e=width),
-                    src[:, a, width * BANK * b : width * BANK * (b + 1)].rearrange("p (q t e) -> p t q e", t=4, e=width),
-                )
-
-        def deal_codes():
-            nc.vector.tensor_copy(
-                a4_dealt[:].bitcast(U16).rearrange("p a (b t q) -> p (a b) t q", b=2, t=4),
-                a4_codes[:].bitcast(U16).rearrange("p a (b q t) -> p (a b) t q", b=2, t=4),
-            )
-
-        def deal_planes(b):
-            deal(a4_dealt_planes[b][:], a4_planes[:].bitcast(U8), b, 1)
-
+        idx = keep.tile([P, S // 16], U16, name="idx")
+        idx2 = keep.tile([P, S // 16], U16, name="idx2")
         wb_rows = wb.rearrange("(p j) r -> p j r", j=4)
-        out_rows = out.rearrange("(c p) s -> p c s", p=P)
 
-        nc.sync.dma_start(v_scale_table[0:32, :], tab_scales.rearrange("a q n -> q a n").bitcast(I32))
+        v_scale_table = held([P, T // 4], I32, "v_scale_table")
+        v2_scale_table = held([P, T // 4], I32, "v2_scale_table")
+        a4_planes = held([P, 2, H // 4], I32, "a4_planes")
+        a4_codes = held([P, 2, H // 2], I32, "a4_codes")
+        v_table = [held([P, T], I32, "v_table0"), held([P, T], I32, "v_table1")]
+        v2_table = held([P, T], I32, "v2_table")
+        v_moved = held([P, 2, S // 4], I32, "v_moved")
+        nc.gpsimd.memset(a4_planes[:], 0)
+        nc.gpsimd.memset(v2_scale_table[:], 0)
         nc.vector.memset(v_scale_table[32:64, :], 0)
         nc.vector.memset(v_scale_table[64:P, :], 0)
-        nc.gpsimd.memset(v2_scale_table[:], 0)
-        nc.gpsimd.memset(a4_planes[:], 0)
-        nc.gpsimd.memset(v_moved[:], 0)
+        nc.vector.memset(v_moved[:], 0)
         nc.sync.dma_start(idx[:], offs)
-        nc.sync.dma_start(idx2[:], offs2)
-        nc.sync.dma_start(v2_table[:], words(tab2_words[0]))
-        for r in range(4):
-            nc.sync.dma_start(v2_scale_table[r:P:32, :], tab2_scales[0, r:16:4, :].bitcast(I32))
-        nc.sync.dma_start(wb_raw[0][:], wb_rows[:, :, 0:BANK])
-        load_planes(a4_planes, a4_scales)
-        nc.sync.dma_start(wb_raw[1][:], wb_rows[:, :, BANK : 2 * BANK])
-        nc.sync.dma_start(a4_codes[:], a4_words.rearrange("a p n -> p a n").bitcast(I32))
+        nc.sync.dma_start(v_scale_table[0:32, :], tab_scales.rearrange("a q n -> q a n").bitcast(I32))
         nc.sync.dma_start(v_table[0][:], words(tab_words[0]))
+        nc.sync.dma_start(a4_codes[:], a4_words.rearrange("a p n -> p a n").bitcast(I32))
+        load_planes(a4_planes, a4_scales)
         nc.sync.dma_start(v_table[1][:], words(tab_words[1]))
+
+        v_scales = held([P, S], U8, "v_scales")
         pick(v_scales[:], v_scale_table[:].bitcast(U8), idx, 0, S)
         for q in range(4):
             nc.sync.dma_start(v_moved[32 * q : 32 * q + 4, :, :], v_scales[8 * q : 8 * q + 8, :].bitcast(I32))
         v_planes = [v_moved[:, a, :].bitcast(U8) for a in range(2)]
+        wb_raw = [held([P, 4, BANK], F32, f"wb_raw{b}") for b in range(2)]
+        nc.sync.dma_start(wb_raw[0][:], wb_rows[:, :, 0:BANK])
+        nc.sync.dma_start(idx2[:], offs2)
+        for r in range(4):
+            nc.sync.dma_start(v2_scale_table[r:P:32, :], tab2_scales[0, r:16:4, :].bitcast(I32))
+        nc.sync.dma_start(v2_table[:], words(tab2_words[0]))
+        nc.sync.dma_start(wb_raw[1][:], wb_rows[:, :, BANK : 2 * BANK])
 
-        pick(v2_codes[:], v2_table[:].bitcast(U32), idx2, 0, S)
-        pick(v2_scales[:], v2_scale_table[:].bitcast(U8), idx2, 0, S)
+        a4_dealt_planes = [held([P, 2, BANK], U8, f"a4_dealt_planes{b}") for b in range(2)]
         for b in range(2):
-            cast(nc.scalar, b, slice(0, 128))
+            for a in range(2):
+                nc.gpsimd.tensor_copy(
+                    a4_dealt_planes[b][:, a, :].rearrange("p (t q) -> p t q", t=4),
+                    a4_planes[:].bitcast(U8)[:, a, BANK * b : BANK * (b + 1)].rearrange("p (q t) -> p t q", t=4),
+                )
+
+        v_codes = [[held([P, HALF], U32, f"v_codes{a}{j}") for j in range(2)] for a in range(2)]
+        pick(v_codes[0][0][:], v_table[0][:].bitcast(U32), idx, 0, HALF)
+        a4_dealt = held([P, 2, H // 2], I32, "a4_dealt")
+        nc.vector.tensor_copy(
+            a4_dealt[:].bitcast(U16).rearrange("p a (b t q) -> p (a b) t q", b=2, t=4),
+            a4_codes[:].bitcast(U16).rearrange("p a (b q t) -> p (a b) t q", b=2, t=4),
+        )
+        pick(v_codes[1][0][:], v_table[1][:].bitcast(U32), idx, 0, HALF)
+        for a in range(2):
+            pick(v_codes[a][1][:], v_table[a][:].bitcast(U32), idx, HALF, HALF)
+
+        wb_grouped = [held([P, BANK, 4], BF16, f"wb_grouped{b}") for b in range(2)]
+        wb_codes = [held([P, BANK], U32, f"wb_codes{b}") for b in range(2)]
+        wb_planes = [held([P, BANK], U8, f"wb_planes{b}") for b in range(2)]
+        for b in range(2):
+            dst = wb_grouped[b][:].rearrange("p (t m) j -> p m t j", t=4)
+            src = wb_raw[b][:].rearrange("p j (m t) -> p m t j", t=4)
+            nc.gpsimd.tensor_scalar(dst, src, 1.0, 0.0, ALU.mult, ALU.add)
+
+        def quantize_wb(b):
             quantize(wb_codes[b][:], wb_planes[b][:], wb_grouped[b][:].rearrange("p n t -> p (n t)"))
-        w8_tile = held([P, 2 * N + N // 2], I32, "w8_tile", "slot5")
+
+        v2_codes = [held([P, HALF], U32, f"v2_codes{j}") for j in range(2)]
+        v2_scales = held([P, S], U8, "v2_scales")
+        pick(v2_scales[:], v2_scale_table[:].bitcast(U8), idx2, 0, S)
+        pick(v2_codes[0][:], v2_table[:].bitcast(U32), idx2, 0, HALF)
+        quantize_wb(0)
+        pick(v2_codes[1][:], v2_table[:].bitcast(U32), idx2, HALF, HALF)
+
+        w8_tile = held([P, 2 * N + N // 2], I32, "w8_tile")
         w8_codes = w8_tile[:, 0 : 2 * N].rearrange("p (a n) -> p a n", a=2)
         w8_planes = w8_tile[:, 2 * N : 2 * N + N // 2].rearrange("p (a n) -> p a n", a=2)
         nc.gpsimd.memset(w8_planes, 0)
         nc.sync.dma_start(w8_codes, w8_words.rearrange("a p n i -> p a (n i)").bitcast(I32))
-        pick(v_codes[0][:], v_table[0][:].bitcast(U32), idx, 0, S)
-        g_table = [held([P, T], F32, f"g_table{c}", f"slot{c}") for c in range(4)]
-        for c in range(3):
+        g_table = [held([P, T], F32, f"g_table{c}") for c in range(4)]
+        nc.sync.dma_start(g_table[0][:], gT[0:P, :])
+        load_planes(w8_planes, w8_scales)
+        for c in range(1, 4):
             nc.sync.dma_start(g_table[c][:], gT[P * c : P * (c + 1), :])
-            if c == 1:
-                load_planes(w8_planes, w8_scales)
-        deal_planes(0)
-        deal_planes(1)
-        deal_codes()
-        for first, count in ((0, CHUNK), (CHUNK, CHUNK), (HALF, HALF)):
-            pick(v_codes[1][:, first : first + count], v_table[1][:].bitcast(U32), idx, first, count)
-        nc.sync.dma_start(g_table[3][:], gT[3 * P : 4 * P, :])
 
-        steps = [(i, b) for b in range(2) for i in range(4)] + [(2 * k + s, b) for k in (2, 3) for b in range(2) for s in range(2)]
-        on_gpsimd = (0, 1, 2, 3, 8, 9, 12, 13)
-        followed = {5: 1, 7: 1, 11: 1}
+        def gate_pass(z, b, t, a, first, count):
+            j = first // HALF
+            rhs = v_codes[a][j][:, first - HALF * j : first - HALF * j + count]
+            nc.tensor.matmul_mx(
+                out=z,
+                lhsT=a4_dealt[:, a, :].bitcast(U8)[:, 2 * (BANK * b + P * t) : 2 * (BANK * b + P * (t + 1))].bitcast(FP4X4),
+                lhsT_scale=a4_dealt_planes[b][:, a, P * t : P * (t + 1)],
+                rhs=rhs.bitcast(FP8X4),
+                rhs_scale=v_planes[a][:, first : first + count],
+                start=(a == 0),
+                stop=(a == 1),
+            )
 
-        def memory(n, tag, bufs):
-            i, b = steps[n]
-            tokens = slice(P * i, P * (i + 1))
-            m = psum.tile([P, 4, P], F32, name="m", tag=tag, bufs=bufs)
+        gates = {}
+
+        def wide_gates(b, j):
+            gates[b, j] = held([P, 4, HALF], F32, f"gate{b}{j}")
+            for t in range(4):
+                z = psum.tile([P, BANK], F32, name="z", tag="sums")
+                for a in range(2):
+                    gate_pass(z[:], b, t, a, HALF * j, HALF)
+                nc.scalar.activation(gates[b, j][:, t, :], z[:], ACT.Sigmoid)
+
+        h_grouped = [held([P, 2, HALF, 4], BF16, f"h_grouped{j}") for j in range(2)]
+        h_codes = [held([P, 2, HALF], U32, f"h_codes{j}") for j in range(2)]
+        h_planes = [held([P, 2, HALF], U8, f"h_planes{j}") for j in range(2)]
+
+        def memory(b, j, i):
+            m = psum.tile([P, 4, P], F32, name="m", tag="m")
             for t in range(4):
                 nc.tensor.matmul_mx(
                     out=m[:, t, :],
                     lhsT=wb_codes[b][:, P * t : P * (t + 1)].bitcast(FP8X4),
                     lhsT_scale=wb_planes[b][:, P * t : P * (t + 1)],
-                    rhs=v2_codes[:, tokens].bitcast(FP8X4),
-                    rhs_scale=v2_scales[:, tokens],
+                    rhs=v2_codes[j][:, P * i : P * (i + 1)].bitcast(FP8X4),
+                    rhs_scale=v2_scales[:, HALF * j + P * i : HALF * j + P * (i + 1)],
                     start=True,
                     stop=True,
                 )
-            return m[:].rearrange("p t n -> p n t")
+            return m
 
-        m_rows = {}
-        for n in on_gpsimd:
-            m_rows[n] = held([P, P, 4], F32, f"m_rows{n}")
-            nc.scalar.copy(m_rows[n][:], memory(n, "sums", 5))
+        def products_on_vector(b, j):
+            for i in range(4):
+                tokens = slice(P * i, P * (i + 1))
+                nc.vector.tensor_tensor(
+                    h_grouped[j][:, b, tokens, :].rearrange("p (c e) t -> p c t e", e=2),
+                    memory(b, j, i)[:].rearrange("p t (c e) -> p c t e", e=2),
+                    gates[b, j][:, :, tokens].rearrange("p t (c e) -> p c t e", e=2),
+                    ALU.mult,
+                )
 
-        def gated_memory(n):
-            i, b = steps[n]
-            tokens = slice(P * i, P * (i + 1))
-            z = psum.tile([P, 4, P], F32, name="z", tag="sums", bufs=5)
+        gate_rows = {}
+
+        def narrow_gate(b, j, i):
+            z = psum.tile([P, 4, P], F32, name="z", tag="sums")
             for t in range(4):
                 for a in range(2):
-                    nc.tensor.matmul_mx(
-                        out=z[:, t, :],
-                        lhsT=a4_dealt[:, a, :].bitcast(U8)[:, 2 * (BANK * b + P * t) : 2 * (BANK * b + P * (t + 1))].bitcast(FP4X4),
-                        lhsT_scale=a4_dealt_planes[b][:, a, P * t : P * (t + 1)],
-                        rhs=v_codes[a][:, tokens].bitcast(FP8X4),
-                        rhs_scale=v_planes[a][:, tokens],
-                        start=(a == 0),
-                        stop=(a == 1),
-                    )
-            if n in followed:
-                sig = held([P, P, 4], F32, f"sig{n}", f"after{n}")
-            else:
-                sig = ring.tile([P, P, 4], F32, name="sig", bufs=10)
-            nc.scalar.activation(sig[:], z[:].rearrange("p t n -> p n t"), ACT.Sigmoid)
-            h = h_grouped[i // 2][:, b, P * (i % 2) : P * (i % 2 + 1), :]
-            if n in on_gpsimd:
-                nc.gpsimd.tensor_tensor(h, m_rows[n][:], sig[:], ALU.mult)
-            else:
-                nc.vector.tensor_tensor(h, memory(n, "m", 3), sig[:], ALU.mult)
+                    gate_pass(z[:, t, :], b, t, a, HALF * j + P * i, P)
+            gate_rows[b, j, i] = held([P, P, 4], F32, f"gate_rows{b}{j}{i}")
+            nc.scalar.activation(gate_rows[b, j, i][:], z[:].rearrange("p t n -> p n t"), ACT.Sigmoid)
 
-        for n in range(16):
-            gated_memory(n)
-            k = steps[n][0] // 2
-            if all(i // 2 != k for i, b in steps[n + 1 :]):
-                if k in h_runs:
-                    codes, planes, grouped = h_runs[k]
-                    quantize(
-                        codes[:].rearrange("p k b n -> p (k b n)"),
-                        planes[:].rearrange("p k b n -> p (k b n)"),
-                        grouped[:].rearrange("p k b n t -> p (k b n t)"),
-                    )
+        def product_on_gpsimd(b, j, i):
+            m_rows = held([P, P, 4], F32, f"m_rows{b}{j}{i}")
+            nc.scalar.copy(m_rows[:], memory(b, j, i)[:].rearrange("p t n -> p n t"))
+            nc.gpsimd.tensor_tensor(h_grouped[j][:, b, P * i : P * (i + 1), :], m_rows[:], gate_rows[b, j, i][:], ALU.mult)
 
-        groups = [held([P, 3, HALF], F32, "g_first")]
-        groups += [held([P, count, HALF], F32, f"g_after{n}", f"after{n}") for n, count in followed.items()]
-        groups += [held([P, 1, HALF], F32, "g_last0", "grouped3"), held([P, 1, HALF], F32, "g_last1", "after5")]
-        places = [group[:, n, :] for group in groups for n in range(group.shape[1])]
-        order = ((0, 0), (1, 0), (0, 1), (1, 1), (0, 2), (0, 3), (1, 2), (1, 3))
-        g_picked = dict(zip(order, places))
-        added_on_vector = ((1, 1), (1, 2), (1, 3))
+        def quantize_h(j):
+            quantize(
+                h_codes[j][:].rearrange("p b n -> p (b n)"),
+                h_planes[j][:].rearrange("p b n -> p (b n)"),
+                h_grouped[j][:].rearrange("p b n t -> p (b n t)"),
+            )
 
-        def leave(j, c):
-            on_vector = (j, c) in added_on_vector
-            acc = psum.tile([P, HALF], F32, name="acc", tag="m" if on_vector else "sums", bufs=3 if on_vector else 5)
-            rows = slice(P * c, P * (c + 1))
-            for s in range(2):
-                k = 2 * j + s
+        wide_gates(0, 0)
+        wide_gates(1, 0)
+        narrow_gate(0, 1, 0)
+        narrow_gate(0, 1, 1)
+        products_on_vector(0, 0)
+        product_on_gpsimd(0, 1, 0)
+        product_on_gpsimd(0, 1, 1)
+        narrow_gate(0, 1, 2)
+        narrow_gate(0, 1, 3)
+        product_on_gpsimd(0, 1, 2)
+        product_on_gpsimd(0, 1, 3)
+        quantize_wb(1)
+        products_on_vector(1, 0)
+        quantize_h(0)
+        wide_gates(1, 1)
+        products_on_vector(1, 1)
+        quantize_h(1)
+
+        for j in range(2):
+            for c in range(4):
+                rows = slice(P * c, P * (c + 1))
+                acc = psum.tile([P, HALF], F32, name="acc", tag="sums")
                 for b in range(2):
                     nc.tensor.matmul_mx(
-                        out=acc[:, CHUNK * s : CHUNK * (s + 1)],
+                        out=acc[:],
                         lhsT=w8_codes[:, b, rows].bitcast(FP8X4),
                         lhsT_scale=w8_planes[:, b, :].bitcast(U8)[:, rows],
-                        rhs=h_codes[k][:, b, :].bitcast(FP8X4),
-                        rhs_scale=h_planes[k][:, b, :],
+                        rhs=h_codes[j][:, b, :].bitcast(FP8X4),
+                        rhs_scale=h_planes[j][:, b, :],
                         start=(b == 0),
                         stop=(b == 1),
                     )
-            cols = slice(HALF * j, HALF * (j + 1))
-            result = ring.tile([P, HALF], F32, name="result", bufs=6)
-            if on_vector:
-                width = CHUNK if (j, c) == order[-1] else HALF
-                for first in range(0, HALF, width):
-                    part = slice(first, first + width)
-                    nc.vector.tensor_tensor(result[:, part], acc[:, part], g_picked[j, c][:, part], ALU.add)
-                    nc.sync.dma_start(out[rows, cols][:, part], result[:, part])
-            else:
                 y = ring.tile([P, HALF], F32, name="y", bufs=4)
                 nc.scalar.copy(y[:], acc[:])
-                nc.gpsimd.tensor_tensor(result[:], y[:], g_picked[j, c], ALU.add)
-                nc.sync.dma_start(out[rows, cols], result[:])
-
-        pick(groups[0][:, 0:2, :].rearrange("p j n -> p (j n)"), g_table[0][:], idx, 0, S)
-        for j, c in order[2:-1]:
-            pick(g_picked[j, c], g_table[c][:], idx, HALF * j, HALF)
-        for j, c in ((0, 0), (0, 1), (0, 2), (0, 3), (1, 1), (1, 0), (1, 2), (1, 3)):
-            if (j, c) == order[-1]:
-                pick(g_picked[j, c], g_table[c][:], idx, HALF * j, HALF)
-            leave(j, c)
+                result = ring.tile([P, HALF], F32, name="result", bufs=4)
+                width = HALF // 2 if (j, c) == (1, 3) else HALF
+                for first in range(0, HALF, width):
+                    part = slice(first, first + width)
+                    start = HALF * j + first
+                    nc.vector.tensor_tensor(
+                        result[:, part], g_table[c][:].indirect(idx[:, start // 16 : (start + width) // 16]), y[:, part], ALU.add
+                    )
+                    nc.sync.dma_start(out[rows, start : start + width], result[:, part])

@@ -28,7 +28,7 @@ def tile_list_paged_memory_gate_kernel(
     with ExitStack() as ctx:
         keep = ctx.enter_context(tc.tile_pool(name="keep", bufs=1))
         ring = ctx.enter_context(tc.tile_pool(name="ring", bufs=4))
-        psum = ctx.enter_context(tc.psum_pool(name="psum", bufs=4))
+        psum = ctx.enter_context(tc.psum_pool(name="psum", bufs=1))
 
         def held(shape, dtype, name, tag=None):
             return keep.tile(shape, dtype, name=name, tag=tag or name, align_bytes=64)
@@ -54,7 +54,8 @@ def tile_list_paged_memory_gate_kernel(
         v_scale_table = held([P, T // 4], I32, "v_scale_table")
         v2_scale_table = held([P, T // 4], I32, "v2_scale_table")
         a4_planes = held([P, 2, H // 4], I32, "a4_planes")
-        a4_codes = held([P, 2, H // 2], I32, "a4_codes")
+        a4_codes = [held([P, 2, BANK // 2], I32, f"a4_codes{b}") for b in range(2)]
+        a4_rows = a4_words.rearrange("a p n -> p a n").bitcast(I32)
         v_table = [held([P, T], I32, "v_table0"), held([P, T], I32, "v_table1")]
         v2_table = held([P, T], I32, "v2_table")
         v_moved = held([P, 2, S // 4], I32, "v_moved")
@@ -65,9 +66,9 @@ def tile_list_paged_memory_gate_kernel(
         nc.vector.memset(v_moved[:], 0)
         nc.sync.dma_start(idx[:], offs)
         nc.sync.dma_start(v_scale_table[0:32, :], tab_scales.rearrange("a q n -> q a n").bitcast(I32))
-        nc.sync.dma_start(v_table[0][:], words(tab_words[0]))
-        nc.sync.dma_start(a4_codes[:], a4_words.rearrange("a p n -> p a n").bitcast(I32))
+        nc.sync.dma_start(a4_codes[0][:], a4_rows[:, :, 0 : BANK // 2])
         load_planes(a4_planes, a4_scales)
+        nc.sync.dma_start(v_table[0][:], words(tab_words[0]))
         nc.sync.dma_start(v_table[1][:], words(tab_words[1]))
 
         v_scales = held([P, S], U8, "v_scales")
@@ -76,6 +77,7 @@ def tile_list_paged_memory_gate_kernel(
             nc.sync.dma_start(v_moved[32 * q : 32 * q + 4, :, :], v_scales[8 * q : 8 * q + 8, :].bitcast(I32))
         v_planes = [v_moved[:, a, :].bitcast(U8) for a in range(2)]
         wb_raw = [held([P, 4, BANK], F32, f"wb_raw{b}") for b in range(2)]
+        nc.sync.dma_start(a4_codes[1][:], a4_rows[:, :, BANK // 2 : BANK])
         nc.sync.dma_start(wb_raw[0][:], wb_rows[:, :, 0:BANK])
         nc.sync.dma_start(idx2[:], offs2)
         for r in range(4):
@@ -84,7 +86,12 @@ def tile_list_paged_memory_gate_kernel(
         nc.sync.dma_start(wb_raw[1][:], wb_rows[:, :, BANK : 2 * BANK])
 
         a4_dealt_planes = [held([P, 2, BANK], U8, f"a4_dealt_planes{b}") for b in range(2)]
+        a4_dealt = [held([P, 2, BANK], U16, f"a4_dealt{b}") for b in range(2)]
         for b in range(2):
+            nc.gpsimd.tensor_copy(
+                a4_dealt[b][:].rearrange("p a (t q) -> p a t q", t=4),
+                a4_codes[b][:].bitcast(U16).rearrange("p a (q t) -> p a t q", t=4),
+            )
             for a in range(2):
                 nc.gpsimd.tensor_copy(
                     a4_dealt_planes[b][:, a, :].rearrange("p (t q) -> p t q", t=4),
@@ -93,11 +100,6 @@ def tile_list_paged_memory_gate_kernel(
 
         v_codes = [[held([P, HALF], U32, f"v_codes{a}{j}") for j in range(2)] for a in range(2)]
         pick(v_codes[0][0][:], v_table[0][:].bitcast(U32), idx, 0, HALF)
-        a4_dealt = held([P, 2, H // 2], I32, "a4_dealt")
-        nc.vector.tensor_copy(
-            a4_dealt[:].bitcast(U16).rearrange("p a (b t q) -> p (a b) t q", b=2, t=4),
-            a4_codes[:].bitcast(U16).rearrange("p a (b q t) -> p (a b) t q", b=2, t=4),
-        )
         pick(v_codes[1][0][:], v_table[1][:].bitcast(U32), idx, 0, HALF)
         for a in range(2):
             pick(v_codes[a][1][:], v_table[a][:].bitcast(U32), idx, HALF, HALF)
@@ -131,12 +133,18 @@ def tile_list_paged_memory_gate_kernel(
         for c in range(1, 4):
             nc.sync.dma_start(g_table[c][:], gT[P * c : P * (c + 1), :])
 
+        turns = {"sums": 0, "m": 0}
+
+        def bank(shape, name, kind):
+            turns.update({kind: turns[kind] + 1})
+            return psum.tile(shape, F32, name=name, tag=f"{kind}{turns[kind] % 4}")
+
         def gate_pass(z, b, t, a, first, count):
             j = first // HALF
             rhs = v_codes[a][j][:, first - HALF * j : first - HALF * j + count]
             nc.tensor.matmul_mx(
                 out=z,
-                lhsT=a4_dealt[:, a, :].bitcast(U8)[:, 2 * (BANK * b + P * t) : 2 * (BANK * b + P * (t + 1))].bitcast(FP4X4),
+                lhsT=a4_dealt[b][:, a, P * t : P * (t + 1)].bitcast(U8).bitcast(FP4X4),
                 lhsT_scale=a4_dealt_planes[b][:, a, P * t : P * (t + 1)],
                 rhs=rhs.bitcast(FP8X4),
                 rhs_scale=v_planes[a][:, first : first + count],
@@ -146,20 +154,20 @@ def tile_list_paged_memory_gate_kernel(
 
         gates = {}
 
-        def wide_gates(b, j):
-            gates[b, j] = held([P, 4, HALF], F32, f"gate{b}{j}")
-            for t in range(4):
-                z = psum.tile([P, BANK], F32, name="z", tag="sums")
-                for a in range(2):
-                    gate_pass(z[:], b, t, a, HALF * j, HALF)
-                nc.scalar.activation(gates[b, j][:, t, :], z[:], ACT.Sigmoid)
+        def wide_gate(b, j, t):
+            if t == 0:
+                gates[b, j] = held([P, 4, HALF], F32, f"gate{b}{j}")
+            z = bank([P, BANK], "z", "sums")
+            for a in range(2):
+                gate_pass(z[:], b, t, a, HALF * j, HALF)
+            nc.scalar.activation(gates[b, j][:, t, :], z[:], ACT.Sigmoid)
 
-        h_grouped = [held([P, 2, HALF, 4], BF16, f"h_grouped{j}") for j in range(2)]
+        h_grouped = [held([P, 2, HALF, 4], BF16, f"h_grouped{j}", f"grouped{j}") for j in range(2)]
         h_codes = [held([P, 2, HALF], U32, f"h_codes{j}") for j in range(2)]
         h_planes = [held([P, 2, HALF], U8, f"h_planes{j}") for j in range(2)]
 
-        def memory(b, j, i):
-            m = psum.tile([P, 4, P], F32, name="m", tag="m")
+        def memory(b, j, i, kind):
+            m = bank([P, 4, P], "m", kind)
             for t in range(4):
                 nc.tensor.matmul_mx(
                     out=m[:, t, :],
@@ -177,7 +185,7 @@ def tile_list_paged_memory_gate_kernel(
                 tokens = slice(P * i, P * (i + 1))
                 nc.vector.tensor_tensor(
                     h_grouped[j][:, b, tokens, :].rearrange("p (c e) t -> p c t e", e=2),
-                    memory(b, j, i)[:].rearrange("p t (c e) -> p c t e", e=2),
+                    memory(b, j, i, "m")[:].rearrange("p t (c e) -> p c t e", e=2),
                     gates[b, j][:, :, tokens].rearrange("p t (c e) -> p c t e", e=2),
                     ALU.mult,
                 )
@@ -185,17 +193,17 @@ def tile_list_paged_memory_gate_kernel(
         gate_rows = {}
 
         def narrow_gate(b, j, i):
-            z = psum.tile([P, 4, P], F32, name="z", tag="sums")
+            z = bank([P, 4, P], "z", "sums")
             for t in range(4):
                 for a in range(2):
                     gate_pass(z[:, t, :], b, t, a, HALF * j + P * i, P)
             gate_rows[b, j, i] = held([P, P, 4], F32, f"gate_rows{b}{j}{i}")
             nc.scalar.activation(gate_rows[b, j, i][:], z[:].rearrange("p t n -> p n t"), ACT.Sigmoid)
 
+        m_rows = [held([P, P, 4], F32, f"m_rows{i}") for i in range(4)]
+
         def product_on_gpsimd(b, j, i):
-            m_rows = held([P, P, 4], F32, f"m_rows{b}{j}{i}")
-            nc.scalar.copy(m_rows[:], memory(b, j, i)[:].rearrange("p t n -> p n t"))
-            nc.gpsimd.tensor_tensor(h_grouped[j][:, b, P * i : P * (i + 1), :], m_rows[:], gate_rows[b, j, i][:], ALU.mult)
+            nc.gpsimd.tensor_tensor(h_grouped[j][:, b, P * i : P * (i + 1), :], m_rows[i][:], gate_rows[b, j, i][:], ALU.mult)
 
         def quantize_h(j):
             quantize(
@@ -204,46 +212,54 @@ def tile_list_paged_memory_gate_kernel(
                 h_grouped[j][:].rearrange("p b n t -> p (b n t)"),
             )
 
-        wide_gates(0, 0)
-        wide_gates(1, 0)
-        narrow_gate(0, 1, 0)
-        narrow_gate(0, 1, 1)
+        ys = {}
+
+        def project(j, c):
+            acc = bank([P, HALF], "acc", "sums")
+            for b in range(2):
+                nc.tensor.matmul_mx(
+                    out=acc[:],
+                    lhsT=w8_codes[:, b, P * c : P * (c + 1)].bitcast(FP8X4),
+                    lhsT_scale=w8_planes[:, b, :].bitcast(U8)[:, P * c : P * (c + 1)],
+                    rhs=h_codes[j][:, b, :].bitcast(FP8X4),
+                    rhs_scale=h_planes[j][:, b, :],
+                    start=(b == 0),
+                    stop=(b == 1),
+                )
+            ys[j, c] = ring.tile([P, HALF], F32, name="y", bufs=4)
+            nc.scalar.copy(ys[j, c][:], acc[:])
+
+        def leave(j, c, result):
+            width = HALF // 2 if (j, c) == (1, 3) else HALF
+            for first in range(0, HALF, width):
+                part = slice(first, first + width)
+                start = HALF * j + first
+                nc.vector.tensor_tensor(
+                    result[:, part], g_table[c][:].indirect(idx[:, start // 16 : (start + width) // 16]), ys[j, c][:, part], ALU.add
+                )
+                nc.sync.dma_start(out[P * c : P * (c + 1), start : start + width], result[:, part])
+
+        for b in range(2):
+            for t in range(4):
+                wide_gate(b, 0, t)
+        for i in range(2):
+            narrow_gate(0, 1, i)
         products_on_vector(0, 0)
-        product_on_gpsimd(0, 1, 0)
-        product_on_gpsimd(0, 1, 1)
+        for i in range(4):
+            nc.scalar.copy(m_rows[i][:], memory(0, 1, i, "sums")[:].rearrange("p t n -> p n t"))
         narrow_gate(0, 1, 2)
-        narrow_gate(0, 1, 3)
-        product_on_gpsimd(0, 1, 2)
-        product_on_gpsimd(0, 1, 3)
+        for i in range(3):
+            product_on_gpsimd(0, 1, i)
         quantize_wb(1)
         products_on_vector(1, 0)
+        narrow_gate(0, 1, 3)
+        product_on_gpsimd(0, 1, 3)
         quantize_h(0)
-        wide_gates(1, 1)
+        for t in range(4):
+            wide_gate(1, 1, t)
         products_on_vector(1, 1)
         quantize_h(1)
-
         for j in range(2):
             for c in range(4):
-                rows = slice(P * c, P * (c + 1))
-                acc = psum.tile([P, HALF], F32, name="acc", tag="sums")
-                for b in range(2):
-                    nc.tensor.matmul_mx(
-                        out=acc[:],
-                        lhsT=w8_codes[:, b, rows].bitcast(FP8X4),
-                        lhsT_scale=w8_planes[:, b, :].bitcast(U8)[:, rows],
-                        rhs=h_codes[j][:, b, :].bitcast(FP8X4),
-                        rhs_scale=h_planes[j][:, b, :],
-                        start=(b == 0),
-                        stop=(b == 1),
-                    )
-                y = ring.tile([P, HALF], F32, name="y", bufs=4)
-                nc.scalar.copy(y[:], acc[:])
-                result = ring.tile([P, HALF], F32, name="result", bufs=4)
-                width = HALF // 2 if (j, c) == (1, 3) else HALF
-                for first in range(0, HALF, width):
-                    part = slice(first, first + width)
-                    start = HALF * j + first
-                    nc.vector.tensor_tensor(
-                        result[:, part], g_table[c][:].indirect(idx[:, start // 16 : (start + width) // 16]), y[:, part], ALU.add
-                    )
-                    nc.sync.dma_start(out[rows, start : start + width], result[:, part])
+                project(j, c)
+                leave(j, c, ring.tile([P, HALF], F32, name="result", bufs=4))

@@ -36,10 +36,10 @@ def tile_list_paged_memory_gate_kernel(
         def words(dram):
             return dram.rearrange("p t i -> p (t i)").bitcast(I32)
 
-        def load_planes(planes, scales):
+        def load_planes(planes, scales, k):
             for r in range(4):
                 rows = scales[:, r:16:4, :].rearrange("a q n -> q a n")
-                nc.sync.dma_start(planes[r:P:32, :, :], rows.bitcast(I32))
+                nc.sync.dma_start(planes[k + r : P : 32, :, :], rows.bitcast(I32))
 
         def pick(dst, table, offsets, first, count):
             nc.vector.tensor_copy(dst, table.indirect(offsets[:, first // 16 : (first + count) // 16]))
@@ -52,9 +52,9 @@ def tile_list_paged_memory_gate_kernel(
         wb_rows = wb.rearrange("(p j) r -> p j r", j=4)
 
         v_scale_table = held([P, T // 4], I32, "v_scale_table")
-        v2_scale_table = held([P, T // 4], I32, "v2_scale_table")
+        v2_scale_table = held([P, T // 4], I32, "v2_scale_table", "scale2")
         a4_planes = held([P, 2, H // 4], I32, "a4_planes")
-        a4_codes = [held([P, 2, BANK // 2], I32, f"a4_codes{b}") for b in range(2)]
+        a4_codes = [held([P, 2, BANK // 2], I32, f"a4_codes{b}", f"packed{b}") for b in range(2)]
         a4_rows = a4_words.rearrange("a p n -> p a n").bitcast(I32)
         v_table = [held([P, T], I32, "v_table0"), held([P, T], I32, "v_table1")]
         v2_table = held([P, T], I32, "v2_table")
@@ -67,7 +67,7 @@ def tile_list_paged_memory_gate_kernel(
         nc.sync.dma_start(idx[:], offs)
         nc.sync.dma_start(v_scale_table[0:32, :], tab_scales.rearrange("a q n -> q a n").bitcast(I32))
         nc.sync.dma_start(a4_codes[0][:], a4_rows[:, :, 0 : BANK // 2])
-        load_planes(a4_planes, a4_scales)
+        load_planes(a4_planes, a4_scales, 0)
         nc.sync.dma_start(v_table[0][:], words(tab_words[0]))
         nc.sync.dma_start(v_table[1][:], words(tab_words[1]))
 
@@ -76,22 +76,18 @@ def tile_list_paged_memory_gate_kernel(
         for q in range(4):
             nc.sync.dma_start(v_moved[32 * q : 32 * q + 4, :, :], v_scales[8 * q : 8 * q + 8, :].bitcast(I32))
         v_planes = [v_moved[:, a, :].bitcast(U8) for a in range(2)]
-        wb_raw = [held([P, 4, BANK], F32, f"wb_raw{b}") for b in range(2)]
+        wb_raw = [held([P, 4, BANK], F32, f"wb_raw{b}", f"raw{b}") for b in range(2)]
         nc.sync.dma_start(a4_codes[1][:], a4_rows[:, :, BANK // 2 : BANK])
         nc.sync.dma_start(wb_raw[0][:], wb_rows[:, :, 0:BANK])
         nc.sync.dma_start(idx2[:], offs2)
         for r in range(4):
-            nc.sync.dma_start(v2_scale_table[r:P:32, :], tab2_scales[0, r:16:4, :].bitcast(I32))
+            nc.sync.dma_start(v2_scale_table[4 + r : P : 32, :], tab2_scales[0, r:16:4, :].bitcast(I32))
         nc.sync.dma_start(v2_table[:], words(tab2_words[0]))
         nc.sync.dma_start(wb_raw[1][:], wb_rows[:, :, BANK : 2 * BANK])
 
         a4_dealt_planes = [held([P, 2, BANK], U8, f"a4_dealt_planes{b}") for b in range(2)]
         a4_dealt = [held([P, 2, BANK], U16, f"a4_dealt{b}") for b in range(2)]
         for b in range(2):
-            nc.gpsimd.tensor_copy(
-                a4_dealt[b][:].rearrange("p a (t q) -> p a t q", t=4),
-                a4_codes[b][:].bitcast(U16).rearrange("p a (q t) -> p a t q", t=4),
-            )
             for a in range(2):
                 nc.gpsimd.tensor_copy(
                     a4_dealt_planes[b][:, a, :].rearrange("p (t q) -> p t q", t=4),
@@ -100,12 +96,20 @@ def tile_list_paged_memory_gate_kernel(
 
         v_codes = [[held([P, HALF], U32, f"v_codes{a}{j}") for j in range(2)] for a in range(2)]
         pick(v_codes[0][0][:], v_table[0][:].bitcast(U32), idx, 0, HALF)
+
+        def deal_codes(b):
+            nc.vector.tensor_copy(
+                a4_dealt[b][:].rearrange("p a (t q) -> p a t q", t=4),
+                a4_codes[b][:].bitcast(U16).rearrange("p a (q t) -> p a t q", t=4),
+            )
+
+        deal_codes(0)
         pick(v_codes[1][0][:], v_table[1][:].bitcast(U32), idx, 0, HALF)
+        deal_codes(1)
         for a in range(2):
             pick(v_codes[a][1][:], v_table[a][:].bitcast(U32), idx, HALF, HALF)
 
-        wb_grouped = [held([P, BANK, 4], BF16, f"wb_grouped{b}") for b in range(2)]
-        wb_codes = [held([P, BANK], U32, f"wb_codes{b}") for b in range(2)]
+        wb_grouped = [held([P, BANK, 4], BF16, f"wb_grouped{b}", "packed1" if b == 0 else None) for b in range(2)]
         wb_planes = [held([P, BANK], U8, f"wb_planes{b}") for b in range(2)]
         for b in range(2):
             dst = wb_grouped[b][:].rearrange("p (t m) j -> p m t j", t=4)
@@ -118,8 +122,9 @@ def tile_list_paged_memory_gate_kernel(
         v2_codes = [held([P, HALF], U32, f"v2_codes{j}") for j in range(2)]
         v2_scales = held([P, S], U8, "v2_scales")
         pick(v2_scales[:], v2_scale_table[:].bitcast(U8), idx2, 0, S)
-        pick(v2_codes[0][:], v2_table[:].bitcast(U32), idx2, 0, HALF)
+        wb_codes = [held([P, BANK], U32, "wb_codes0", "scale2"), held([P, BANK], U32, "wb_codes1")]
         quantize_wb(0)
+        pick(v2_codes[0][:], v2_table[:].bitcast(U32), idx2, 0, HALF)
         pick(v2_codes[1][:], v2_table[:].bitcast(U32), idx2, HALF, HALF)
 
         w8_tile = held([P, 2 * N + N // 2], I32, "w8_tile")
@@ -129,15 +134,12 @@ def tile_list_paged_memory_gate_kernel(
         nc.sync.dma_start(w8_codes, w8_words.rearrange("a p n i -> p a (n i)").bitcast(I32))
         g_table = [held([P, T], F32, f"g_table{c}") for c in range(4)]
         nc.sync.dma_start(g_table[0][:], gT[0:P, :])
-        load_planes(w8_planes, w8_scales)
+        load_planes(w8_planes, w8_scales, 8)
         for c in range(1, 4):
             nc.sync.dma_start(g_table[c][:], gT[P * c : P * (c + 1), :])
 
-        turns = {"sums": 0, "m": 0}
-
-        def bank(shape, name, kind):
-            turns.update({kind: turns[kind] + 1})
-            return psum.tile(shape, F32, name=name, tag=f"{kind}{turns[kind] % 4}")
+        def bank(shape, name, n):
+            return psum.tile(shape, F32, name=name, tag=f"bank{n}")
 
         def gate_pass(z, b, t, a, first, count):
             j = first // HALF
@@ -157,24 +159,24 @@ def tile_list_paged_memory_gate_kernel(
         def wide_gate(b, j, t):
             if t == 0:
                 gates[b, j] = held([P, 4, HALF], F32, f"gate{b}{j}")
-            z = bank([P, BANK], "z", "sums")
+            z = bank([P, BANK], "z", t if (b, j) == (0, 0) else 4 + t)
             for a in range(2):
                 gate_pass(z[:], b, t, a, HALF * j, HALF)
             nc.scalar.activation(gates[b, j][:, t, :], z[:], ACT.Sigmoid)
 
-        h_grouped = [held([P, 2, HALF, 4], BF16, f"h_grouped{j}", f"grouped{j}") for j in range(2)]
+        h_grouped = [held([P, 2, HALF, 4], BF16, f"h_grouped{j}", "raw1" if j == 1 else None) for j in range(2)]
         h_codes = [held([P, 2, HALF], U32, f"h_codes{j}") for j in range(2)]
         h_planes = [held([P, 2, HALF], U8, f"h_planes{j}") for j in range(2)]
 
-        def memory(b, j, i, kind):
-            m = bank([P, 4, P], "m", kind)
+        def memory(b, j, i):
+            m = bank([P, 4, P], "m", (i + 2) % 4 if (b, j) == (0, 1) else 4 + i)
             for t in range(4):
                 nc.tensor.matmul_mx(
                     out=m[:, t, :],
                     lhsT=wb_codes[b][:, P * t : P * (t + 1)].bitcast(FP8X4),
                     lhsT_scale=wb_planes[b][:, P * t : P * (t + 1)],
                     rhs=v2_codes[j][:, P * i : P * (i + 1)].bitcast(FP8X4),
-                    rhs_scale=v2_scales[:, HALF * j + P * i : HALF * j + P * (i + 1)],
+                    rhs_scale=v2_scales[4:P, HALF * j + P * i : HALF * j + P * (i + 1)],
                     start=True,
                     stop=True,
                 )
@@ -185,7 +187,7 @@ def tile_list_paged_memory_gate_kernel(
                 tokens = slice(P * i, P * (i + 1))
                 nc.vector.tensor_tensor(
                     h_grouped[j][:, b, tokens, :].rearrange("p (c e) t -> p c t e", e=2),
-                    memory(b, j, i, "m")[:].rearrange("p t (c e) -> p c t e", e=2),
+                    memory(b, j, i)[:].rearrange("p t (c e) -> p c t e", e=2),
                     gates[b, j][:, :, tokens].rearrange("p t (c e) -> p c t e", e=2),
                     ALU.mult,
                 )
@@ -193,7 +195,7 @@ def tile_list_paged_memory_gate_kernel(
         gate_rows = {}
 
         def narrow_gate(b, j, i):
-            z = bank([P, 4, P], "z", "sums")
+            z = bank([P, 4, P], "z", i)
             for t in range(4):
                 for a in range(2):
                     gate_pass(z[:, t, :], b, t, a, HALF * j + P * i, P)
@@ -215,12 +217,12 @@ def tile_list_paged_memory_gate_kernel(
         ys = {}
 
         def project(j, c):
-            acc = bank([P, HALF], "acc", "sums")
+            acc = bank([P, HALF], "acc", 4 * j + c)
             for b in range(2):
                 nc.tensor.matmul_mx(
                     out=acc[:],
                     lhsT=w8_codes[:, b, P * c : P * (c + 1)].bitcast(FP8X4),
-                    lhsT_scale=w8_planes[:, b, :].bitcast(U8)[:, P * c : P * (c + 1)],
+                    lhsT_scale=w8_planes[8:P, b, :].bitcast(U8)[:, P * c : P * (c + 1)],
                     rhs=h_codes[j][:, b, :].bitcast(FP8X4),
                     rhs_scale=h_planes[j][:, b, :],
                     start=(b == 0),
@@ -246,14 +248,13 @@ def tile_list_paged_memory_gate_kernel(
             narrow_gate(0, 1, i)
         products_on_vector(0, 0)
         for i in range(4):
-            nc.scalar.copy(m_rows[i][:], memory(0, 1, i, "sums")[:].rearrange("p t n -> p n t"))
-        narrow_gate(0, 1, 2)
-        for i in range(3):
+            nc.scalar.copy(m_rows[i][:], memory(0, 1, i)[:].rearrange("p t n -> p n t"))
+        for i in range(2, 4):
+            narrow_gate(0, 1, i)
+        for i in range(4):
             product_on_gpsimd(0, 1, i)
         quantize_wb(1)
         products_on_vector(1, 0)
-        narrow_gate(0, 1, 3)
-        product_on_gpsimd(0, 1, 3)
         quantize_h(0)
         for t in range(4):
             wide_gate(1, 1, t)

@@ -76,7 +76,7 @@ def tile_list_paged_memory_gate_kernel(
         for q in range(4):
             nc.sync.dma_start(v_moved[32 * q : 32 * q + 4, :, :], v_scales[8 * q : 8 * q + 8, :].bitcast(I32))
         v_planes = [v_moved[:, a, :].bitcast(U8) for a in range(2)]
-        wb_raw = [held([P, 4, BANK], F32, f"wb_raw{b}", f"raw{b}") for b in range(2)]
+        wb_raw = [held([P, 4, BANK], F32, f"wb_raw{b}") for b in range(2)]
         nc.sync.dma_start(a4_codes[1][:], a4_rows[:, :, BANK // 2 : BANK])
         nc.sync.dma_start(wb_raw[0][:], wb_rows[:, :, 0:BANK])
         nc.sync.dma_start(idx2[:], offs2)
@@ -109,7 +109,7 @@ def tile_list_paged_memory_gate_kernel(
         for a in range(2):
             pick(v_codes[a][1][:], v_table[a][:].bitcast(U32), idx, HALF, HALF)
 
-        wb_grouped = [held([P, BANK, 4], BF16, f"wb_grouped{b}", "packed1" if b == 0 else None) for b in range(2)]
+        wb_grouped = [held([P, BANK, 4], BF16, f"wb_grouped{b}", "packed1" if b == 0 else "rounded1") for b in range(2)]
         wb_planes = [held([P, BANK], U8, f"wb_planes{b}") for b in range(2)]
         for b in range(2):
             dst = wb_grouped[b][:].rearrange("p (t m) j -> p m t j", t=4)
@@ -164,8 +164,10 @@ def tile_list_paged_memory_gate_kernel(
                 gate_pass(z[:], b, t, a, HALF * j, HALF)
             nc.scalar.activation(gates[b, j][:, t, :], z[:], ACT.Sigmoid)
 
-        h_grouped = [held([P, 2, HALF, 4], BF16, f"h_grouped{j}", "raw1" if j == 1 else None) for j in range(2)]
-        h_codes = [held([P, 2, HALF], U32, f"h_codes{j}") for j in range(2)]
+        h_first = held([P, 2, HALF, 4], BF16, "h_first", "first")
+        h_last = held([P, HALF, 4], BF16, "h_last")
+        h_grouped = {(0, 0): h_first[:, 0], (1, 0): h_first[:, 1], (1, 1): h_last[:]}
+        h_codes = {1: held([P, 2, HALF], U32, "h_codes1")}
         h_planes = [held([P, 2, HALF], U8, f"h_planes{j}") for j in range(2)]
 
         def memory(b, j, i):
@@ -186,7 +188,7 @@ def tile_list_paged_memory_gate_kernel(
             for i in range(4):
                 tokens = slice(P * i, P * (i + 1))
                 nc.vector.tensor_tensor(
-                    h_grouped[j][:, b, tokens, :].rearrange("p (c e) t -> p c t e", e=2),
+                    h_grouped[b, j][:, tokens, :].rearrange("p (c e) t -> p c t e", e=2),
                     memory(b, j, i)[:].rearrange("p t (c e) -> p c t e", e=2),
                     gates[b, j][:, :, tokens].rearrange("p t (c e) -> p c t e", e=2),
                     ALU.mult,
@@ -204,15 +206,15 @@ def tile_list_paged_memory_gate_kernel(
 
         m_rows = [held([P, P, 4], F32, f"m_rows{i}") for i in range(4)]
 
-        def product_on_gpsimd(b, j, i):
-            nc.gpsimd.tensor_tensor(h_grouped[j][:, b, P * i : P * (i + 1), :], m_rows[i][:], gate_rows[b, j, i][:], ALU.mult)
+        def products_on_gpsimd(first, tag):
+            h_pair = held([P, 2, P, 4], BF16, f"h_pair{first}", tag)
+            for i in range(2):
+                nc.gpsimd.tensor_tensor(h_pair[:, i], m_rows[first + i][:], gate_rows[0, 1, first + i][:], ALU.mult)
+            return h_pair
 
-        def quantize_h(j):
-            quantize(
-                h_codes[j][:].rearrange("p b n -> p (b n)"),
-                h_planes[j][:].rearrange("p b n -> p (b n)"),
-                h_grouped[j][:].rearrange("p b n t -> p (b n t)"),
-            )
+        def quantize_pair(k):
+            part = slice(2 * P * k, 2 * P * (k + 1))
+            quantize(h_codes[1][:, 0, part], h_planes[1][:, 0, part], pairs[k][:].rearrange("p i n t -> p (i n t)"))
 
         ys = {}
 
@@ -251,15 +253,22 @@ def tile_list_paged_memory_gate_kernel(
             nc.scalar.copy(m_rows[i][:], memory(0, 1, i)[:].rearrange("p t n -> p n t"))
         for i in range(2, 4):
             narrow_gate(0, 1, i)
-        for i in range(4):
-            product_on_gpsimd(0, 1, i)
         quantize_wb(1)
+        pairs = [products_on_gpsimd(0, "rounded1")]
         products_on_vector(1, 0)
-        quantize_h(0)
+        quantize_pair(0)
+        h_codes[0] = held([P, 2, HALF], U32, "h_codes0", "rounded1")
+        quantize(
+            h_codes[0][:].rearrange("p b n -> p (b n)"),
+            h_planes[0][:].rearrange("p b n -> p (b n)"),
+            h_first[:].rearrange("p b n t -> p (b n t)"),
+        )
+        pairs.append(products_on_gpsimd(2, "first"))
         for t in range(4):
             wide_gate(1, 1, t)
         products_on_vector(1, 1)
-        quantize_h(1)
+        quantize(h_codes[1][:, 1, :], h_planes[1][:, 1, :], h_last[:].rearrange("p n t -> p (n t)"))
+        quantize_pair(1)
         for j in range(2):
             for c in range(4):
                 project(j, c)

@@ -164,10 +164,8 @@ def tile_list_paged_memory_gate_kernel(
                 gate_pass(z[:], b, t, a, HALF * j, HALF)
             nc.scalar.activation(gates[b, j][:, t, :], z[:], ACT.Sigmoid)
 
-        h_first = held([P, 2, HALF, 4], BF16, "h_first", "first")
-        h_last = held([P, HALF, 4], BF16, "h_last")
-        h_grouped = {(0, 0): h_first[:, 0], (1, 0): h_first[:, 1], (1, 1): h_last[:]}
-        h_codes = {1: held([P, 2, HALF], U32, "h_codes1")}
+        h_grouped = {(b, j): held([P, HALF, 4], BF16, f"h{b}{j}")[:] for b, j in ((0, 0), (1, 0), (1, 1))}
+        h_codes = {(b, 1): held([P, HALF], U32, f"h_codes{b}1") for b in range(2)}
         h_planes = [held([P, 2, HALF], U8, f"h_planes{j}") for j in range(2)]
 
         def memory(b, j, i):
@@ -194,27 +192,25 @@ def tile_list_paged_memory_gate_kernel(
                     ALU.mult,
                 )
 
-        gate_rows = {}
+        gate_rows = [held([P, 2, P, 4], F32, f"gate_rows{k}") for k in range(2)]
 
         def narrow_gate(b, j, i):
             z = bank([P, 4, P], "z", i)
             for t in range(4):
                 for a in range(2):
                     gate_pass(z[:, t, :], b, t, a, HALF * j + P * i, P)
-            gate_rows[b, j, i] = held([P, P, 4], F32, f"gate_rows{b}{j}{i}")
-            nc.scalar.activation(gate_rows[b, j, i][:], z[:].rearrange("p t n -> p n t"), ACT.Sigmoid)
+            nc.scalar.activation(gate_rows[i // 2][:, i % 2], z[:].rearrange("p t n -> p n t"), ACT.Sigmoid)
 
-        m_rows = [held([P, P, 4], F32, f"m_rows{i}") for i in range(4)]
+        m_rows = [held([P, 2, P, 4], F32, f"m_rows{k}") for k in range(2)]
 
-        def products_on_gpsimd(first, tag):
-            h_pair = held([P, 2, P, 4], BF16, f"h_pair{first}", tag)
-            for i in range(2):
-                nc.gpsimd.tensor_tensor(h_pair[:, i], m_rows[first + i][:], gate_rows[0, 1, first + i][:], ALU.mult)
+        def products_on_gpsimd(k, tag):
+            h_pair = held([P, 2, P, 4], BF16, f"h_pair{k}", tag)
+            nc.gpsimd.tensor_tensor(h_pair[:], m_rows[k][:], gate_rows[k][:], ALU.mult)
             return h_pair
 
         def quantize_pair(k):
             part = slice(2 * P * k, 2 * P * (k + 1))
-            quantize(h_codes[1][:, 0, part], h_planes[1][:, 0, part], pairs[k][:].rearrange("p i n t -> p (i n t)"))
+            quantize(h_codes[0, 1][:, part], h_planes[1][:, 0, part], pairs[k][:].rearrange("p i n t -> p (i n t)"))
 
         ys = {}
 
@@ -225,7 +221,7 @@ def tile_list_paged_memory_gate_kernel(
                     out=acc[:],
                     lhsT=w8_codes[:, b, P * c : P * (c + 1)].bitcast(FP8X4),
                     lhsT_scale=w8_planes[8:P, b, :].bitcast(U8)[:, P * c : P * (c + 1)],
-                    rhs=h_codes[j][:, b, :].bitcast(FP8X4),
+                    rhs=h_codes[b, j][:].bitcast(FP8X4),
                     rhs_scale=h_planes[j][:, b, :],
                     start=(b == 0),
                     stop=(b == 1),
@@ -250,24 +246,26 @@ def tile_list_paged_memory_gate_kernel(
             narrow_gate(0, 1, i)
         products_on_vector(0, 0)
         for i in range(4):
-            nc.scalar.copy(m_rows[i][:], memory(0, 1, i)[:].rearrange("p t n -> p n t"))
+            nc.scalar.copy(m_rows[i // 2][:, i % 2], memory(0, 1, i)[:].rearrange("p t n -> p n t"))
         for i in range(2, 4):
             narrow_gate(0, 1, i)
+
+        def quantize_h(b, j):
+            quantize(h_codes[b, j][:], h_planes[j][:, b, :], h_grouped[b, j].rearrange("p n t -> p (n t)"))
+
         quantize_wb(1)
-        pairs = [products_on_gpsimd(0, "rounded1")]
+        h_codes[0, 0] = held([P, HALF], U32, "h_codes00", "rounded1")
+        quantize_h(0, 0)
+        pairs = [products_on_gpsimd(0, "h00")]
         products_on_vector(1, 0)
         quantize_pair(0)
-        h_codes[0] = held([P, 2, HALF], U32, "h_codes0", "rounded1")
-        quantize(
-            h_codes[0][:].rearrange("p b n -> p (b n)"),
-            h_planes[0][:].rearrange("p b n -> p (b n)"),
-            h_first[:].rearrange("p b n t -> p (b n t)"),
-        )
-        pairs.append(products_on_gpsimd(2, "first"))
+        h_codes[1, 0] = held([P, HALF], U32, "h_codes10", "h00")
+        quantize_h(1, 0)
+        pairs.append(products_on_gpsimd(1, "h10"))
         for t in range(4):
             wide_gate(1, 1, t)
         products_on_vector(1, 1)
-        quantize(h_codes[1][:, 1, :], h_planes[1][:, 1, :], h_last[:].rearrange("p n t -> p (n t)"))
+        quantize_h(1, 1)
         quantize_pair(1)
         for j in range(2):
             for c in range(4):

@@ -97,15 +97,15 @@ def tile_list_paged_memory_gate_kernel(
         v_codes = [[held([P, HALF], U32, f"v_codes{a}{j}") for j in range(2)] for a in range(2)]
         pick(v_codes[0][0][:], v_table[0][:].bitcast(U32), idx, 0, HALF)
 
-        def deal_codes(b):
-            nc.vector.tensor_copy(
+        def deal_codes(b, copy):
+            copy(
                 a4_dealt[b][:].rearrange("p a (t q) -> p a t q", t=4),
                 a4_codes[b][:].bitcast(U16).rearrange("p a (q t) -> p a t q", t=4),
             )
 
-        deal_codes(0)
+        deal_codes(0, nc.scalar.copy)
         pick(v_codes[1][0][:], v_table[1][:].bitcast(U32), idx, 0, HALF)
-        deal_codes(1)
+        deal_codes(1, nc.vector.tensor_copy)
         for a in range(2):
             pick(v_codes[a][1][:], v_table[a][:].bitcast(U32), idx, HALF, HALF)
 

@@ -169,7 +169,7 @@ def tile_list_paged_memory_gate_kernel(
         h_planes = [held([P, 2, HALF], U8, f"h_planes{j}") for j in range(2)]
 
         def memory(b, j, i):
-            m = bank([P, 4, P], "m", (i + 2) % 4 if (b, j) == (0, 1) else 4 + i)
+            m = bank([P, 4, P], "m", 4 + i if j == 0 else (i + 2) % 4)
             for t in range(4):
                 nc.tensor.matmul_mx(
                     out=m[:, t, :],
@@ -188,18 +188,20 @@ def tile_list_paged_memory_gate_kernel(
                 nc.vector.tensor_tensor(
                     h_grouped[b, j][:, tokens, :].rearrange("p (c e) t -> p c t e", e=2),
                     memory(b, j, i)[:].rearrange("p t (c e) -> p c t e", e=2),
-                    gates[b, j][:, :, tokens].rearrange("p t (c e) -> p c t e", e=2),
+                    gates[b, 0][:, :, tokens].rearrange("p t (c e) -> p c t e", e=2)
+                    if j == 0
+                    else gate_rows[2 + i // 2][:, i % 2].rearrange("p (c e) t -> p c t e", e=2),
                     ALU.mult,
                 )
 
-        gate_rows = [held([P, 2, P, 4], F32, f"gate_rows{k}") for k in range(2)]
+        gate_rows = [held([P, 2, P, 4], F32, f"gate_rows{k}") for k in range(4)]
 
         def narrow_gate(b, j, i):
-            z = bank([P, 4, P], "z", i)
+            z = bank([P, 4, P], "z", 4 * b + i)
             for t in range(4):
                 for a in range(2):
                     gate_pass(z[:, t, :], b, t, a, HALF * j + P * i, P)
-            nc.scalar.activation(gate_rows[i // 2][:, i % 2], z[:].rearrange("p t n -> p n t"), ACT.Sigmoid)
+            nc.scalar.activation(gate_rows[2 * b + i // 2][:, i % 2], z[:].rearrange("p t n -> p n t"), ACT.Sigmoid)
 
         m_rows = [held([P, 2, P, 4], F32, f"m_rows{k}") for k in range(2)]
 
@@ -215,7 +217,7 @@ def tile_list_paged_memory_gate_kernel(
         ys = {}
 
         def project(j, c):
-            acc = bank([P, HALF], "acc", 4 * j + c)
+            acc = bank([P, HALF], "acc", 4 * (1 - j) + c)
             for b in range(2):
                 nc.tensor.matmul_mx(
                     out=acc[:],
@@ -262,8 +264,8 @@ def tile_list_paged_memory_gate_kernel(
         h_codes[1, 0] = held([P, HALF], U32, "h_codes10", "h00")
         quantize_h(1, 0)
         pairs.append(products_on_gpsimd(1, "h10"))
-        for t in range(4):
-            wide_gate(1, 1, t)
+        for i in range(4):
+            narrow_gate(1, 1, i)
         products_on_vector(1, 1)
         quantize_h(1, 1)
         quantize_pair(1)

from contextlib import ExitStack

import concourse.mybir as mybir

K, C, H, N, T, S = 1024, 512, 1024, 512, 2048, 1024
FLOPS = 2 * S * H * (K + C + N)

F32 = mybir.dt.float32
BF16 = mybir.dt.bfloat16
I32 = mybir.dt.int32
U32 = mybir.dt.uint32
U16 = mybir.dt.uint16
U8 = mybir.dt.uint8
FP8X4 = mybir.dt.float8_e4m3fn_x4
FP4X4 = mybir.dt.float4_e2m1fn_x4
ACT = mybir.ActivationFunctionType
ALU = mybir.AluOpType

P = 128
BANK = 512
HALF = 512


def tile_list_paged_memory_gate_kernel(
    tc, tab_words, tab_scales, tab2_words, tab2_scales, a4_words, a4_scales, wb, w8_words, w8_scales, gT, offs, offs2, out
):
    nc = tc.nc
    with ExitStack() as ctx:
        keep = ctx.enter_context(tc.tile_pool(name="keep", bufs=1))
        ring = ctx.enter_context(tc.tile_pool(name="ring", bufs=4))
        psum = ctx.enter_context(tc.psum_pool(name="psum", bufs=1))

        def held(shape, dtype, name, tag=None):
            return keep.tile(shape, dtype, name=name, tag=tag or name, align_bytes=64)

        def words(dram):
            return dram.rearrange("p t i -> p (t i)").bitcast(I32)

        def load_planes(planes, scales, k):
            for r in range(4):
                rows = scales[:, r:16:4, :].rearrange("a q n -> q a n")
                nc.sync.dma_start(planes[k + r : P : 32, :, :], rows.bitcast(I32))

        def pick(dst, table, offsets, first, count):
            nc.vector.tensor_copy(dst, table.indirect(offsets[:, first // 16 : (first + count) // 16]))

        def quantize(codes, planes, grouped):
            nc.vector.quantize_mx(out=codes.bitcast(FP8X4), scales=planes, in_=grouped)

        idx = keep.tile([P, S // 16], U16, name="idx")
        idx2 = keep.tile([P, S // 16], U16, name="idx2")
        wb_rows = wb.rearrange("(p j) r -> p j r", j=4)

        v_scale_table = held([P, T // 4], I32, "v_scale_table")
        v2_scale_table = held([P, T // 4], I32, "v2_scale_table", "scale2")
        a4_planes = held([P, 2, H // 4], I32, "a4_planes")
        a4_codes = [held([P, 2, BANK // 2], I32, f"a4_codes{b}", f"packed{b}") for b in range(2)]
        a4_rows = a4_words.rearrange("a p n -> p a n").bitcast(I32)
        v_table = [held([P, T], I32, "v_table0"), held([P, T], I32, "v_table1")]
        v2_table = held([P, T], I32, "v2_table")
        v_moved = held([P, 2, S // 4], I32, "v_moved")
        nc.gpsimd.memset(a4_planes[:], 0)
        nc.gpsimd.memset(v2_scale_table[:], 0)
        nc.vector.memset(v_scale_table[32:64, :], 0)
        nc.vector.memset(v_scale_table[64:P, :], 0)
        nc.vector.memset(v_moved[:], 0)
        nc.sync.dma_start(idx[:], offs)
        nc.sync.dma_start(v_scale_table[0:32, :], tab_scales.rearrange("a q n -> q a n").bitcast(I32))
        nc.sync.dma_start(a4_codes[0][:], a4_rows[:, :, 0 : BANK // 2])
        load_planes(a4_planes, a4_scales, 0)
        nc.sync.dma_start(v_table[0][:], words(tab_words[0]))
        nc.sync.dma_start(v_table[1][:], words(tab_words[1]))

        v_scales = held([P, S], U8, "v_scales")
        pick(v_scales[:], v_scale_table[:].bitcast(U8), idx, 0, S)
        for q in range(4):
            nc.sync.dma_start(v_moved[32 * q : 32 * q + 4, :, :], v_scales[8 * q : 8 * q + 8, :].bitcast(I32))
        v_planes = [v_moved[:, a, :].bitcast(U8) for a in range(2)]
        wb_raw = [held([P, 4, BANK], F32, f"wb_raw{b}") for b in range(2)]
        nc.sync.dma_start(a4_codes[1][:], a4_rows[:, :, BANK // 2 : BANK])
        nc.sync.dma_start(wb_raw[0][:], wb_rows[:, :, 0:BANK])
        nc.sync.dma_start(idx2[:], offs2)
        for r in range(4):
            nc.sync.dma_start(v2_scale_table[4 + r : P : 32, :], tab2_scales[0, r:16:4, :].bitcast(I32))
        nc.sync.dma_start(v2_table[:], words(tab2_words[0]))
        nc.sync.dma_start(wb_raw[1][:], wb_rows[:, :, BANK : 2 * BANK])

        a4_dealt_planes = [held([P, 2, BANK], U8, f"a4_dealt_planes{b}") for b in range(2)]
        a4_dealt = [held([P, 2, BANK], U16, f"a4_dealt{b}") for b in range(2)]
        for b in range(2):
            for a in range(2):
                nc.gpsimd.tensor_copy(
                    a4_dealt_planes[b][:, a, :].rearrange("p (t q) -> p t q", t=4),
                    a4_planes[:].bitcast(U8)[:, a, BANK * b : BANK * (b + 1)].rearrange("p (q t) -> p t q", t=4),
                )

        v_codes = [[held([P, HALF], U32, f"v_codes{a}{j}") for j in range(2)] for a in range(2)]
        pick(v_codes[0][0][:], v_table[0][:].bitcast(U32), idx, 0, HALF)

        def deal_codes(b, copy):
            copy(
                a4_dealt[b][:].rearrange("p a (t q) -> p a t q", t=4),
                a4_codes[b][:].bitcast(U16).rearrange("p a (q t) -> p a t q", t=4),
            )

        deal_codes(0, nc.scalar.copy)
        pick(v_codes[1][0][:], v_table[1][:].bitcast(U32), idx, 0, HALF)
        deal_codes(1, nc.vector.tensor_copy)
        for a in range(2):
            pick(v_codes[a][1][:], v_table[a][:].bitcast(U32), idx, HALF, HALF)

        wb_grouped = [held([P, BANK, 4], BF16, f"wb_grouped{b}", "packed1" if b == 0 else "rounded1") for b in range(2)]
        wb_planes = [held([P, BANK], U8, f"wb_planes{b}") for b in range(2)]
        for b in range(2):
            dst = wb_grouped[b][:].rearrange("p (t m) j -> p m t j", t=4)
            src = wb_raw[b][:].rearrange("p j (m t) -> p m t j", t=4)
            nc.gpsimd.tensor_scalar(dst, src, 1.0, 0.0, ALU.mult, ALU.add)

        def quantize_wb(b):
            quantize(wb_codes[b][:], wb_planes[b][:], wb_grouped[b][:].rearrange("p n t -> p (n t)"))

        v2_codes = [held([P, HALF], U32, f"v2_codes{j}") for j in range(2)]
        v2_scales = held([P, S], U8, "v2_scales")
        pick(v2_scales[:], v2_scale_table[:].bitcast(U8), idx2, 0, S)
        wb_codes = [held([P, BANK], U32, "wb_codes0", "scale2"), held([P, BANK], U32, "wb_codes1")]
        quantize_wb(0)
        pick(v2_codes[0][:], v2_table[:].bitcast(U32), idx2, 0, HALF)
        pick(v2_codes[1][:], v2_table[:].bitcast(U32), idx2, HALF, HALF)

        w8_tile = held([P, 2 * N + N // 2], I32, "w8_tile")
        w8_codes = w8_tile[:, 0 : 2 * N].rearrange("p (a n) -> p a n", a=2)
        w8_planes = w8_tile[:, 2 * N : 2 * N + N // 2].rearrange("p (a n) -> p a n", a=2)
        nc.gpsimd.memset(w8_planes, 0)
        nc.sync.dma_start(w8_codes, w8_words.rearrange("a p n i -> p a (n i)").bitcast(I32))
        g_table = [held([P, T], F32, f"g_table{c}") for c in range(4)]
        nc.sync.dma_start(g_table[0][:], gT[0:P, :])
        load_planes(w8_planes, w8_scales, 8)
        for c in range(1, 4):
            nc.sync.dma_start(g_table[c][:], gT[P * c : P * (c + 1), :])

        def bank(shape, name, n):
            return psum.tile(shape, F32, name=name, tag=f"bank{n}")

        def gate_pass(z, b, t, a, first, count):
            j = first // HALF
            rhs = v_codes[a][j][:, first - HALF * j : first - HALF * j + count]
            nc.tensor.matmul_mx(
                out=z,
                lhsT=a4_dealt[b][:, a, P * t : P * (t + 1)].bitcast(U8).bitcast(FP4X4),
                lhsT_scale=a4_dealt_planes[b][:, a, P * t : P * (t + 1)],
                rhs=rhs.bitcast(FP8X4),
                rhs_scale=v_planes[a][:, first : first + count],
                start=(a == 0),
                stop=(a == 1),
            )

        gates = {}

        def wide_gate(b, j, t):
            if t == 0:
                gates[b, j] = held([P, 4, HALF], F32, f"gate{b}{j}")
            z = bank([P, BANK], "z", t if (b, j) == (0, 0) else 4 + t)
            for a in range(2):
                gate_pass(z[:], b, t, a, HALF * j, HALF)
            nc.scalar.activation(gates[b, j][:, t, :], z[:], ACT.Sigmoid)

        h_grouped = {(b, j): held([P, HALF, 4], BF16, f"h{b}{j}")[:] for b, j in ((0, 0), (1, 0), (1, 1))}
        h_codes = {(b, 1): held([P, HALF], U32, f"h_codes{b}1") for b in range(2)}
        h_planes = [held([P, 2, HALF], U8, f"h_planes{j}") for j in range(2)]

        def memory(b, j, i):
            m = bank([P, 4, P], "m", 4 + i if j == 0 else (i + 2) % 4)
            for t in range(4):
                nc.tensor.matmul_mx(
                    out=m[:, t, :],
                    lhsT=wb_codes[b][:, P * t : P * (t + 1)].bitcast(FP8X4),
                    lhsT_scale=wb_planes[b][:, P * t : P * (t + 1)],
                    rhs=v2_codes[j][:, P * i : P * (i + 1)].bitcast(FP8X4),
                    rhs_scale=v2_scales[4:P, HALF * j + P * i : HALF * j + P * (i + 1)],
                    start=True,
                    stop=True,
                )
            return m

        def products_on_vector(b, j):
            for i in range(4):
                tokens = slice(P * i, P * (i + 1))
                nc.vector.tensor_tensor(
                    h_grouped[b, j][:, tokens, :].rearrange("p (c e) t -> p c t e", e=2),
                    memory(b, j, i)[:].rearrange("p t (c e) -> p c t e", e=2),
                    gates[b, 0][:, :, tokens].rearrange("p t (c e) -> p c t e", e=2)
                    if j == 0
                    else gate_rows[2 + i // 2][:, i % 2].rearrange("p (c e) t -> p c t e", e=2),
                    ALU.mult,
                )

        gate_rows = [held([P, 2, P, 4], F32, f"gate_rows{k}") for k in range(4)]

        def narrow_gate(b, j, i):
            z = bank([P, 4, P], "z", 4 * b + i)
            for t in range(4):
                for a in range(2):
                    gate_pass(z[:, t, :], b, t, a, HALF * j + P * i, P)
            nc.scalar.activation(gate_rows[2 * b + i // 2][:, i % 2], z[:].rearrange("p t n -> p n t"), ACT.Sigmoid)

        m_rows = [held([P, 2, P, 4], F32, f"m_rows{k}") for k in range(2)]

        def products_on_gpsimd(k, tag):
            h_pair = held([P, 2, P, 4], BF16, f"h_pair{k}", tag)
            nc.gpsimd.tensor_tensor(h_pair[:], m_rows[k][:], gate_rows[k][:], ALU.mult)
            return h_pair

        def quantize_pair(k):
            part = slice(2 * P * k, 2 * P * (k + 1))
            quantize(h_codes[0, 1][:, part], h_planes[1][:, 0, part], pairs[k][:].rearrange("p i n t -> p (i n t)"))

        ys = {}

        def project(j, c):
            acc = bank([P, HALF], "acc", 4 * (1 - j) + c)
            for b in range(2):
                nc.tensor.matmul_mx(
                    out=acc[:],
                    lhsT=w8_codes[:, b, P * c : P * (c + 1)].bitcast(FP8X4),
                    lhsT_scale=w8_planes[8:P, b, :].bitcast(U8)[:, P * c : P * (c + 1)],
                    rhs=h_codes[b, j][:].bitcast(FP8X4),
                    rhs_scale=h_planes[j][:, b, :],
                    start=(b == 0),
                    stop=(b == 1),
                )
            ys[j, c] = ring.tile([P, HALF], F32, name="y", bufs=4)
            nc.scalar.copy(ys[j, c][:], acc[:])

        def leave(j, c, result):
            width = HALF // 2 if (j, c) == (1, 3) else HALF
            for first in range(0, HALF, width):
                part = slice(first, first + width)
                start = HALF * j + first
                nc.vector.tensor_tensor(
                    result[:, part], g_table[c][:].indirect(idx[:, start // 16 : (start + width) // 16]), ys[j, c][:, part], ALU.add
                )
                nc.sync.dma_start(out[P * c : P * (c + 1), start : start + width], result[:, part])

        for b in range(2):
            for t in range(4):
                wide_gate(b, 0, t)
        for i in range(2):
            narrow_gate(0, 1, i)
        products_on_vector(0, 0)
        for i in range(4):
            nc.scalar.copy(m_rows[i // 2][:, i % 2], memory(0, 1, i)[:].rearrange("p t n -> p n t"))
        for i in range(2, 4):
            narrow_gate(0, 1, i)

        def quantize_h(b, j):
            quantize(h_codes[b, j][:], h_planes[j][:, b, :], h_grouped[b, j].rearrange("p n t -> p (n t)"))

        quantize_wb(1)
        h_codes[0, 0] = held([P, HALF], U32, "h_codes00", "rounded1")
        quantize_h(0, 0)
        pairs = [products_on_gpsimd(0, "h00")]
        products_on_vector(1, 0)
        quantize_pair(0)
        h_codes[1, 0] = held([P, HALF], U32, "h_codes10", "h00")
        quantize_h(1, 0)
        pairs.append(products_on_gpsimd(1, "h10"))
        for i in range(4):
            narrow_gate(1, 1, i)
        products_on_vector(1, 1)
        quantize_h(1, 1)
        quantize_pair(1)
        for j in range(2):
            for c in range(4):
                project(j, c)
                leave(j, c, ring.tile([P, HALF], F32, name="result", bufs=4))
